import numpy as np, ml_dtypes
CORES = [40,41,42,43,44,45,46,47]
N = 8
BF = ml_dtypes.bfloat16
def gentries(a):
    return np.ascontiguousarray(a.reshape(8, 16, -1).transpose(0, 2, 1)).reshape(8, -1)
def gtable(e):
    e = np.asarray(e); return np.ascontiguousarray(e.reshape(8, -1, 16).transpose(0, 2, 1)).reshape(128, -1).astype(np.int32)
W, L, M, B, TS, CAP = 8192, 512, 2, 4, 4, 128
R = M * B
KAPPA = (3, 29)
def run(x, z, v):
    tr = []
    for b in range(B):
        u = np.add.reduce(z, axis=2)
        c = np.concatenate([((u * u >> 4) + k * u + v) & (W - 1) for k in KAPPA], axis=2)
        y = np.take_along_axis(x, c[:, :, None, :], 3).reshape(N, 8, 16, M, L)
        z = np.abs(np.maximum.reduce(y, axis=3) - z)
        tr.append(c)
    return z, np.concatenate(tr, axis=2)
def starts(z, h, fr):
    halt = (~fr) & (np.add.reduce((z >= h[..., None]).astype(np.int64), axis=2) >= 9)
    slot = np.add.accumulate(halt.astype(np.int64), axis=2) - halt
    return halt & (slot < CAP)
def parts(rng):
    return rng.integers(0, 256, (N, 8, 16, W)), rng.integers(0, 256, (N, 8, 16, L)), rng.integers(0, W, (N, 8, L))
def levels(rng, x, s, v, share):
    j = rng.integers(-24, 25, (N, 8, 16, TS)); z = run(x, s, v)[0]; th = np.zeros((N, 8, 16, TS), np.int64)
    for t in range(TS):
        k = np.sort(np.sort(z - j[..., t:t + 1], axis=2)[:, :, 7], axis=2)
        n = np.minimum(np.maximum((share[..., t] * L).astype(np.int64), 1), L)
        th[..., t] = np.take_along_axis(k, (L - n)[..., None], 2) + j[..., t]
    return np.minimum(np.maximum(th, 0), 255)
def pack(x, s, v, th):
    return {"x": x.reshape(N, 128, W).astype(np.float32).astype(BF), "sd": s.reshape(N, 128, L).astype(np.float32).astype(BF),
            "v0": np.stack([gtable(a) for a in v]), "th": np.ascontiguousarray(th.reshape(N, 128, TS)).astype(np.int32)}
def shares(rng):
    return rng.choice(np.array([0.1, 0.25, 0.4, 0.6]), (N, 8, TS))
def setup_inputs(rng):
    x, s, v = parts(rng)
    return pack(x, s, v, levels(rng, x, s, v, shares(rng)))
def setup_inputs_claims(rng):
    x, s, v = parts(rng); share = rng.choice(np.array([0.2, 0.35, 0.45]), (N, 8, TS)); th = levels(rng, x, s, v, share)
    z, c = run(x, s, v); go = starts(z, th[..., 0], np.zeros((N, 8, L), bool))
    for r in range(0, N, 2):
        for g in range(8):
            j = np.nonzero(go[r + 1, g])[0]
            if len(j) == 0: j = np.arange(L)
            e = rng.choice(np.array([0, R - 1, -1]), L); e = np.where(e < 0, rng.integers(0, R, L), e)
            v[r, g] = np.where(rng.random(L) < 0.6, c[r + 1, g, e * L + rng.choice(j, L)], v[r, g])
    th[0::2] = levels(rng, x, s, v, share)[0::2]
    th[1, :, :, 1] = 255; th[:, 5, :, 2] = 255; th[2, :, :, TS - 1] = 255
    return pack(x, s, v, th)
def setup_inputs_corners(rng):
    x, s, v = parts(rng); v = np.ascontiguousarray(np.argsort(rng.random((N, 8, W)), axis=-1)[..., :L])
    pm = np.ones((N, 8), bool); pm[2:, 6:] = False
    x = np.where(pm[:, :, None, None], 255, x)
    n = rng.choice(np.array([0, 1, CAP - 1, CAP, CAP + 1, L]), (N, 8)); n[0] = 0
    n[1] = np.array([CAP, CAP + 1, L, CAP, L, CAP + 1, CAP, L]); n[2] = np.array([CAP, CAP + 1, L, CAP - 1, 1, 0, CAP, CAP])
    hot = np.argsort(np.argsort(rng.random((N, 8, L)), axis=2), axis=2) < n[:, :, None]
    k = np.where(hot, np.where(rng.random((N, 8, L)) < 0.5, 9, rng.integers(9, 17, (N, 8, L))), np.where(rng.random((N, 8, L)) < 0.5, 8, rng.integers(0, 9, (N, 8, L))))
    up = np.argsort(np.argsort(rng.random((N, 8, 16, L)), axis=2), axis=2) < k[:, :, None, :]
    tb = rng.integers(1, 256, (N, 8, 16)); tb[:, 1] = 1; tb[:, 3] = 255; tb[:, 5] = rng.choice(np.array([1, 255]), (N, 16))
    b = tb[..., None]; near = rng.random(s.shape) < 0.5
    hi = np.where(near, b, b + ((256 - b) * rng.random(s.shape)).astype(np.int64)); lo = np.where(near, b - 1, (b * rng.random(s.shape)).astype(np.int64))
    s = np.where(pm[:, :, None, None], np.where(up, hi, lo), s)
    th = levels(rng, x, s, v, shares(rng)); th[..., 0] = np.where(pm[:, :, None], tb, th[..., 0])
    return pack(x, s, v, th)
def setup_inputs_ends(rng):
    x, s, v = parts(rng); one = 1.0
    for i in range(M.bit_length() - 1): one = one * 0.5
    a = rng.random((N, 8, 1, W)); x = np.where(a < 0.4 * one, 255, np.where(a < 1.2 * one, 255 * rng.integers(0, 2, x.shape), 0))
    a = rng.random((N, 8, 1, L)); s = np.where(a < 0.35, 255, np.where(a < 0.6, 0, 255 * rng.integers(0, 2, s.shape)))
    v = np.where(rng.random(v.shape) < 0.72, (W - 1) * rng.integers(0, 2, v.shape), v)
    x[:, 1::2, :, W - 1] = 255; x[:, 0::2, :, W - 1] = 0; x[:, :, :, 0] = 255 - x[:, :, :, W - 1]
    s[:, 1::2, :, L - 1] = 255; s[:, 0::2, :, L - 1] = 0; s[:, :, :, 0] = 255 - s[:, :, :, L - 1]; s[:, 1::2, :, 5] = 255; s[:, 1::2, :, L - 4] = 255
    v[:, :, L - 1] = W - 1; v[:, :, L - 4] = W - 1; v[:, :, 5] = W - 1; v[:, :, 0] = 0
    k = rng.choice(np.array([16, 16, 12, 10, 9, 8, 8, 7, 0]), (N, 8, 1, TS)); k[:, 7, :, 0] = 12; k[:, 6, :, 0] = 0; k[:, 0, :, TS - 1] = 9; k[:, 7, :, TS - 1] = 16
    th = np.where(np.argsort(np.argsort(rng.random((N, 8, 16, TS)), axis=2), axis=2) < k, 255, 0)
    return pack(x, s, v, th)
def setup_inputs_spread(rng):
    x, s, v = parts(rng)
    x = np.minimum((np.exp2(1 + 7 * rng.random((N, 8, 1, W))) * rng.random(x.shape)).astype(np.int64), 255)
    s = np.minimum((np.exp2(1 + 7 * rng.random((N, 8, 1, L))) * rng.random(s.shape)).astype(np.int64), 255)
    v = np.minimum((W * rng.random(v.shape) ** 3).astype(np.int64), W - 1)
    return pack(x, s, v, levels(rng, x, s, v, shares(rng)))
def setup_inputs_ties(rng):
    x, s, v = parts(rng); pool = rng.integers(0, W, (8, 12)); pool[:, 0] = 0; pool[:, 1] = W - 1; h = L // 2; q = L // 4
    v = np.stack([pool[g][rng.integers(0, 12, (N, L))] for g in range(8)], axis=1)
    s[..., h:] = s[..., :h]; v[..., h:] = np.where(rng.random((N, 8, h)) < 0.5, v[..., :h], v[..., h:])
    pl = [2, 4, 7]; x[:, 2] = 255; x[:, 4] = 0; x[:, 7] = 0
    s[:, pl] = rng.integers(0, 100, (N, 3, 16, L))
    for a in range(0, N, 2):
        b = a + 1
        k = int(rng.integers(1, 4)); p = int(v[b, 2, 0])
        s[b, 2, :, k * q:(k + 1) * q] = 255; v[b, 2, k * q:(k + 1) * q] = p
        s[a, 2, :, (k - 1) * q:k * q] = rng.integers(201, 256, (16, q))
        v[a, 2, (k - 1) * q:k * q] = np.where(rng.random(q) < 0.8, p, v[a, 2, (k - 1) * q:k * q]); v[a, 2, (k - 1) * q] = p
        ln = np.append(q + rng.permutation(3 * q - 1)[:3], L - 1); e = rng.integers(201, 252, 4); pv = 16 * rng.permutation(W // 16)[:4] + 1; u = 16 * e
        s[b, 4][:, ln] = e; v[b, 4][ln] = pv
        wr = rng.permutation(q)[:4 * M]; s[a, 4][:, wr] = rng.integers(201, 252, 4 * M); s[a, 4][5, wr] += 4
        v[a, 4][wr] = np.concatenate([((u * u >> 4) + m * u + pv) & (W - 1) for m in KAPPA])
        p = W - 2 if a == 0 else int(rng.integers(W // 2, W - 1))
        for l, c in ((0, p + 1), (h, p)):
            s[b, 7, :, l] = rng.integers(201, 256, 16); u = int(np.sum(s[b, 7, :, l])); v[b, 7, l] = (c - (u * u >> 4) - KAPPA[0] * u) & (W - 1)
        for l, c in ((3, p + 1), (L - 1, p)):
            s[a, 7, :, l] = rng.integers(201, 256, 16); v[a, 7, l] = c
    th = levels(rng, x, s, v, shares(rng)); th[..., 0][:, pl] = rng.integers(100, 201, (N, 3, 16))
    return pack(x, s, v, th)
def check_inputs(d):
    bad = []
    for k, lo, hi in (("x", 0, 255), ("sd", 0, 255), ("v0", 0, W - 1), ("th", 0, 255)):
        a = np.asarray(d[k]).astype(np.float64)
        if not (np.min(a) >= lo and np.max(a) <= hi): bad.append("range of " + k)
        elif np.any(np.floor(a) != a): bad.append("whole numbers in " + k)
    return bad
def reference(x, sd, v0, th):
    X = x.astype(np.float32).astype(np.int64).reshape(N, 8, 16, W); S = sd.astype(np.float32).astype(np.int64).reshape(N, 8, 16, L)
    H = th.astype(np.int64).reshape(N, 8, 16, TS); v = np.stack([gentries(a) for a in v0]).astype(np.int64)
    fr = np.zeros((N, 8, L), bool); tr = np.zeros((N, 8, R * L), np.int64); cl = np.arange(L) * 4 // L
    for t in range(TS):
        z, c = run(X, S, v)
        tr = np.where(np.tile(fr, (1, 1, R)), tr, c)
        go = starts(z, H[..., t], fr); fr = fr | go
        back = np.zeros((N, 8, L), bool); hurt = np.zeros((N, 8, L), bool); done = np.zeros((N, 1, 1), np.int64)
        for q in range(N):
            p = q ^ (1 + t % (N - 1))
            for g in range(8):
                ln = np.nonzero(go[p, g])[0]; w = v[p, g, ln]
                mark = np.full(W, 9); np.minimum.at(mark, tr[q, g], np.where(np.tile(fr[q, g], R), np.tile(cl, R), 9))
                ok = np.nonzero(mark[w] > cl[ln])[0]
                win = np.zeros(len(ln), bool); win[ok[np.unique(w[ok], return_index=True)[1]]] = True
                back[p, g, ln[~win]] = True; done[q, 0, 0] += np.count_nonzero(win)
                if t < TS - 1: X[q, g][:, w[win]] = z[p, g][:, ln[win]]
                hit = np.zeros(W, bool); hit[w[win]] = True
                hurt[q, g] = fr[q, g] & np.any(hit[tr[q, g]].reshape(R, L), axis=0)
        fr = fr & (~back) & (~hurt)
        v = np.where(fr, v, (((v & 4095) ** 2 >> 3) + 37 * v + done) & (W - 1))
    ys = np.concatenate([v, fr.astype(np.int64)], axis=2)
    return {"yt": np.stack([gtable(a) for a in tr]).astype(np.float32), "ys": np.stack([gtable(a) for a in ys]).astype(np.float32)}

@@ -1,0 +1,602 @@
+from concourse.mybir import AluOpType as ALU, AxisListType, ActivationFunctionType as AF
+
+W, L, TS = 8192, 512, 4
+KS = (3, 29)
+NM = 8320
+
+SCRATCH = {
+    "X": ("sbuf", [128, NM], "bfloat16"), "MAP": ("sbuf", [128, NM], "bfloat16"),
+    "SEL": ("sbuf", [128, 2048], "bfloat16"), "EI": ("sbuf", [128, 2048], "bfloat16"),
+    "SD": ("sbuf", [128, 512], "bfloat16"), "V0": ("sbuf", [128, 32], "int32"), "THI": ("sbuf", [128, 4], "int32"),
+    "KL": ("sbuf", [128, 512], "float32"), "KWS": ("sbuf", [128, 32], "float32"), "KWL": ("sbuf", [128, 32], "float32"),
+    "ZS": ("sbuf", [128, 384], "bfloat16"), "ZL": ("sbuf", [128, 384], "bfloat16"),
+    "NDS": ("sbuf", [128, 512], "bfloat16"), "NDL": ("sbuf", [128, 512], "bfloat16"),
+    "G": ("sbuf", [128, 4096], "bfloat16"), "HG": ("sbuf", [128, 4096], "bfloat16"),
+    "LO": ("sbuf", [128, 4096], "bfloat16"), "HI": ("sbuf", [128, 2048], "bfloat16"),
+    "KX": ("sbuf", [128, 512], "float32"), "KEYR": ("sbuf", [128, 512], "float32"),
+    "YT": ("sbuf", [128, 256], "float32"), "YS": ("sbuf", [128, 64], "float32"),
+    "PF": ("sbuf", [128, 6000], "float32"), "PI": ("sbuf", [128, 3000], "int32"),
+    "PU": ("sbuf", [128, 1000], "uint16"), "PB": ("sbuf", [128, 12000], "bfloat16"),
+}
+for _t in range(TS): SCRATCH["KSD%d" % _t] = ("sbuf", [128, 1536], "float32")
+PSUM = ("U0", "D0", "D1", "TPA", "TPB", "HP", "BD")
+for _b in PSUM: SCRATCH[_b] = ("psum", [128, 512], "float32")
+QUEUES = ("pe", "dve", "act", "gp")
+SEMAPHORES = (["c_" + q for q in QUEUES] + ["ld_x", "ld_sd", "ld_v", "ld_th", "st_t", "st_s", "lsem"]
+              + ["%s%d" % (k, t) for k in ("rk", "rw", "rz", "rb") for t in range(TS)])
+
+CYC, PEC, HOP = 0.001, 0.00086, 0.1
+ORDER = {}
+CFG = {"map": ((1, 2), (1, 3, 4, 7), (1, 3, 4, 10), (1, 3, 9, 10, 12, 14)),
+       "hg": ((0, 3), (1, 2, 4, 5), (2, 3, 4, 5, 7, 9, 11), (0, 2, 4, 6, 10, 11, 13, 14)),
+       "sp": 4, "kw": 3, "kx": 16, "lg": 1, "span": [0.0]}
+
+
+def dv(n, c=1.0):
+    return max(64, n * c) * CYC
+
+
+def gat(n):
+    return 0.066 + 1.56 * n * CYC
+
+
+def sca(n):
+    return 0.06 + 3.8 * n * CYC
+
+
+def rank_program(g, core, T, topo):
+    rank = T.rank_of(core)
+    if rank is None:
+        return
+    ops = []
+    acc = {}
+    pool = {"PF": [0], "PI": [0], "PU": [0], "PB": [0]}
+
+    def op(eng, fn, reads, writes, dur, event=None, after=(), lat=0.0, early=False):
+        n = len(ops)
+        deps = {}
+
+        def need(m, wait):
+            deps[m] = deps.get(m, False) or wait
+        for (b, lo, hi) in reads:
+            ex = b in PSUM
+            for (l2, h2, m, wr) in acc.get(b, []):
+                over = l2 < hi and lo < h2
+                if over or ex:
+                    same = ops[m]["eng"] == eng
+                    if wr: need(m, over if same else True)
+                    elif ex: need(m, not same)
+        for (b, lo, hi) in writes:
+            ex = b in PSUM
+            for (l2, h2, m, wr) in acc.get(b, []):
+                if l2 < hi and lo < h2 or ex:
+                    need(m, ops[m]["eng"] != eng or eng in ("sp", "net"))
+        for m in after: need(m, False)
+        ops.append({"eng": eng, "fn": fn, "deps": deps, "dur": dur, "event": event, "lat": lat, "early": early})
+        for (b, lo, hi) in reads:
+            acc.setdefault(b, []).append((lo, hi, n, False))
+        for (b, lo, hi) in writes:
+            if b in PSUM: keep = [a for a in acc.get(b, []) if ops[a[2]]["eng"] == eng and a[3]][-40:]
+            else: keep = [a for a in acc.get(b, []) if not (lo <= a[0] and a[1] <= hi)]
+            acc[b] = keep + [(lo, hi, n, True)]
+        return n
+
+    def al(p, n):
+        a = pool[p][0]
+        pool[p][0] = a + (n + 15) // 16 * 16
+        assert pool[p][0] <= SCRATCH[p][1][1], p
+        return (p, a, a + n)
+
+    def two(p, n):
+        return (al(p, n), al(p, n))
+
+    def ap(r):
+        return T[r[0]][:, r[1]:r[2]] if len(r) == 3 else T[r[0]][:, r[1]:r[2]:r[3]]
+
+    def rg(r):
+        return (r[0], r[1], r[2])
+
+    def sub(r, lo, hi, st=None):
+        return (r[0], r[1] + lo, r[1] + hi) if st is None else (r[0], r[1] + lo, r[1] + hi, st)
+
+    def wd(r):
+        return r[2] - r[1] if len(r) == 3 else (r[2] - r[1] + r[3] - 1) // r[3]
+
+    def fastc(*rs):
+        return 0.5 if all(SCRATCH[r[0]][2] in ("bfloat16", "uint16") and r[0] not in PSUM for r in rs) else 1.0
+
+    def copy(o, i):
+        op("dve", lambda: g.vector.tensor_copy(out=ap(o), in_=ap(i)), [rg(i)], [rg(o)], dv(wd(o), fastc(o, i)))
+
+    def tt(o, a, b, f):
+        c = 1.0 if (a[0] in PSUM or b[0] in PSUM) else 2.0
+        op("dve", lambda: g.vector.tensor_tensor(out=ap(o), in0=ap(a), in1=ap(b), op=f), [rg(a), rg(b)], [rg(o)], dv(wd(o), c))
+
+    def ts(o, a, s1, f1, s2=None, f2=None):
+        rd = [rg(a)] + [rg(s) for s in (s1, s2) if isinstance(s, tuple)]
+
+        def fn():
+            x1 = ap(s1) if isinstance(s1, tuple) else s1
+            x2 = ap(s2) if isinstance(s2, tuple) else s2
+            if f2 is None:
+                return g.vector.tensor_scalar(out=ap(o), in0=ap(a), scalar1=x1, scalar2=None, op0=f1)
+            return g.vector.tensor_scalar(out=ap(o), in0=ap(a), scalar1=x1, scalar2=x2, op0=f1, op1=f2)
+        op("dve", fn, rd, [rg(o)], dv(wd(o), fastc(o, a)))
+
+    def fill(o, v):
+        op("dve", lambda: g.vector.memset(ap(o), v), [], [rg(o)], dv(wd(o), fastc(o)), early=128 < wd(o) < 8000)
+
+    def red(o, a, f):
+        op("dve", lambda: g.vector.tensor_reduce(out=ap(o), in_=ap(a), axis=AxisListType.X, op=f), [rg(a)], [rg(o)], dv(wd(a)))
+
+    def ind(win, off):
+        return T[win[0]][:, win[1]:win[2]].indirect(ap(off))
+
+    def scatter(win, off, src):
+        op("dve", lambda: g.vector.tensor_copy(out=ind(win, off), in_=ap(src)), [rg(off), rg(src)], [rg(win)], sca(wd(src)))
+
+    def gather(eng, o, win, off):
+        if eng == "act": fn = lambda: g.scalar.activation(out=ap(o), in_=ind(win, off), func=AF.Copy)
+        else: fn = lambda: g.vector.tensor_copy(out=ap(o), in_=ind(win, off))
+        op(eng, fn, [rg(win), rg(off)], [rg(o)], gat(wd(o)))
+
+    def act(o, a, f, bias=None, scale=None, acc_o=None):
+        rd = [rg(a)] + [rg(r) for r in (bias, scale) if r is not None]
+
+        def fn():
+            kw = {}
+            if bias is not None: kw["bias"] = ap(bias)
+            if scale is not None: kw["scale"] = ap(scale)
+            if acc_o is not None: kw["accum_out"] = ap(acc_o)
+            return g.scalar.activation(out=ap(o), in_=ap(a), func=f, **kw)
+        op("act", fn, rd, [rg(o)] + ([rg(acc_o)] if acc_o is not None else []), dv(wd(o)) + (0.02 if acc_o is not None else 0.0))
+
+    def mm(lst, f32=False, p8=False):
+        rd, wr = [], []
+        d = 0.0
+        for (o, a, b, s0, s1) in lst:
+            for r in (a, b):
+                if rg(r) not in rd: rd.append(rg(r))
+            if rg(o) not in wr: wr.append(rg(o))
+            d += max(min(64, wd(a)), wd(b)) * PEC * (4 if f32 else 1)
+
+        def fn():
+            x = None
+            for (o, a, b, s0, s1) in lst:
+                x = g.tensor.matmul(T[o[0]][0:8, o[1]:o[2]] if p8 else ap(o), ap(a), ap(b), s0, s1)
+            return x
+        op("pe", fn, rd, wr, d)
+
+    def iota(o, pat, base, cm):
+        op("gp", lambda: g.iota(ap(o), pat, base, cm, allow_small_or_imprecise_dtypes=True), [], [rg(o)], 0.15 + 2 * wd(o) * CYC)
+
+    def asel(o, a, pat, cmp, base, cm):
+        op("gp", lambda: g.affine_select(ap(o), ap(a), pat, cmp, 0.0, base, cm), [rg(a)], [rg(o)], 0.2 + 2 * wd(o) * CYC)
+
+    used = [0]
+
+    def send(dst, o, i, sem, lat):
+        rid, pid, _ = topo.addr(dst)
+        en = topo.engines(core, dst)[::2]
+        m = sum(1 << e for e in en)
+        used[0] += len(en)
+
+        def fn():
+            g.remote_dma(ap(o), ap(i), T.sem[sem], T.sem.lsem, pid, rid, m)
+        s = op("gp", fn, [rg(i)], [], 0.1)
+        op("net", None, [], [rg(o)], 0.0, event=(sem, len(en)), after=(s,), lat=lat)
+
+    def dma(o_ap, i_ap, rd, wr, sem, lat):
+        op("sp", lambda: g.sync.dma_start(o_ap, i_ap).then_inc(T.sem[sem], 16), rd, wr, 0.1, event=(sem, 16), lat=lat)
+
+    V0, THI, SD, XW = ("V0", 0, 32), ("THI", 0, 4), ("SD", 0, 512), ("X", 0, W)
+    dma(T.V0[:], T.v0[:], [], [V0], "ld_v", 2.0)
+    dma(T.SD[:], T.sd[:], [], [SD], "ld_sd", 2.5)
+    dma(T.X[:, 0:W], T.x[:], [], [XW], "ld_x", 10.0)
+    dma(T.THI[:], T.th[:], [], [THI], "ld_th", 3.0)
+
+    ONE, BO, t0, ID = al("PB", 128), al("PB", 128), al("PB", 128), al("PB", 128)
+    fill(ONE, 1.0)
+    asel(t0, ONE, [[-16, 8], [0, 16]], ALU.is_ge, 0, 1)
+    asel(BO, t0, [[16, 8], [0, 16]], ALU.is_ge, 15, -1)
+    asel(ID, ONE, [[-1, 128]], ALU.is_equal, 0, 1)
+    fill(("SEL", 0, 2048), 0.0)
+    for i in range(16): copy(("SEL", i * 128 + i, (i + 1) * 128, 16), sub(BO, i, 128, 16))
+
+    def sel(i):
+        return ("SEL", i * 128, (i + 1) * 128)
+    NID, NID16 = al("PB", 128), al("PB", 128)
+    ts(NID, ID, -1.0, ALU.mult)
+    ts(NID16, ID, -16.0, ALU.mult)
+    BIAS = (al("PF", 1), al("PF", 1))
+    for m in range(2): fill(BIAS[m], 8.0 * KS[m])
+    h1, h2, M16 = al("PF", 64), al("PF", 32), al("PF", 16)
+    tt(h1, sub(ID, 0, 64), sub(ID, 64, 128), ALU.add)
+    tt(h2, sub(h1, 0, 32), sub(h1, 32, 64), ALU.add)
+    tt(M16, sub(h2, 0, 16), sub(h2, 16, 32), ALU.add)
+
+    def m16(i):
+        return sub(M16, i, i + 1)
+    i16, x16, IC = al("PF", 16), al("PF", 16), al("PF", 1)
+    iota(i16, [[1, 16]], 0, 0)
+    tt(x16, M16, i16, ALU.mult)
+    red(IC, x16, ALU.add)
+    INI, iq, LANE, TL, P16N = al("PF", 1), al("PF", 32), al("PF", 32), al("PF", 32), al("PF", 32)
+    ts(INI, IC, 512.0 - 16.0, ALU.add)
+    iota(iq, [[16, 32]], 0, 0)
+    ts(LANE, iq, IC, ALU.add)
+    ts(TL, LANE, 512.0, ALU.add)
+    fill(P16N, 16.0)
+    V16 = al("PF", 64)
+
+    def v16ops(dst, src):
+        for m in range(2): ts(sub(dst, m * 32, m * 32 + 32), src, 16.0, ALU.mult, -64.0 * KS[m] ** 2, ALU.add)
+    v16ops(V16, V0)
+
+    def sums(zr, extra=None):
+        o = ("U0", 0, 32)
+        lst = [(o, NID16, extra, True, False)] if extra is not None else []
+        for i in range(16): lst.append((o, sel(i), sub(zr, i, 512, 16), extra is None and i == 0, i == 15))
+        mm(lst)
+        return o
+    SQ0 = al("PF", 64)
+    o = sums(SD)
+    for m in range(2): act(sub(SQ0, m * 32, m * 32 + 32), o, AF.Square, BIAS[m])
+
+    MAP = ("MAP", 0, NM)
+    fill(MAP, 0.0)
+    TH = al("PF", 4)
+    copy(TH, THI)
+    TRI, nbo, BOF = al("PB", 128), al("PB", 128), al("PF", 128)
+    ts(nbo, BO, -1.0, ALU.mult)
+    asel(TRI, nbo, [[-1, 128]], ALU.is_ge, 0, 1)
+    copy(BOF, BO)
+    for i in range(16): ts(("EI", i * 128, i * 128 + 128), BO, m16(i), ALU.mult)
+    RHE, RK = al("PB", 64), al("PB", 24)
+    for k in range(8): ts(sub(RHE, k * 8, k * 8 + 8), sub(BO, 0, 128, 16), m16(0), ALU.mult)
+    for k in range(3): ts(sub(RK, k, 24, 3), sub(BO, 0, 128, 16), m16(k), ALU.mult)
+    ex0, EXP, KT = al("PB", 128), al("PB", 128), al("PB", 512)
+    asel(ex0, ONE, [[1, 128]], ALU.is_ge, 0, -16)
+    asel(EXP, ex0, [[-1, 128]], ALU.is_ge, 15, 16)
+    DM, DG = al("PF", 128), al("PF", 64)
+    for k in range(8): copy(sub(DM, k * 16, k * 16 + 16), M16)
+    copy(DG, sub(BO, 0, 128, 2))
+    i8, TRW, SROW = al("PF", 8), al("PF", 8), al("PF", 128)
+    iota(i8, [[16, 8]], W, 0)
+    ts(TRW, i8, IC, ALU.add)
+    iota(SROW, [[1024, 128]], W * 1024 + 896, 0)
+    for t in range(TS): copy(("KSD%d" % t, 0, 128), SROW)
+    hir, lor, hm2, lm2, SC = al("PF", 128), al("PF", 128), al("PF", 128), al("PF", 128), al("PB", 128)
+    iota(hir, [[1, 8], [0, 16]], 1, 0)
+    iota(lor, [[0, 8], [1, 16]], 1, 0)
+    ts(hm2, hir, m16(0), ALU.mult)
+    ts(lm2, lor, m16(1), ALU.mult)
+    tt(SC, hm2, lm2, ALU.add)
+    KRP, P16, N16, ZERO = al("PB", 512), al("PB", 128), al("PB", 128), al("PB", 128)
+    fill(KRP, 0.0)
+    fill(P16, 16.0)
+    fill(N16, -16.0)
+    fill(ZERO, 0.0)
+
+    SQ, SI, C16, Y1, HB = two("PF", 64), two("PI", 64), two("PU", 64), two("PB", 512), two("PB", 512)
+    ZH, ZF, GE = al("PB", 1536), al("PB", 512), al("PB", 512)
+    CN, TM = two("PI", 256), two("PF", 256)
+    tda, tdb = al("PF", 256), al("PF", 256)
+    OFF, CLX = al("PU", 256), al("PF", 256)
+    ZG, SQS, VSE, SIS, CS, VSW = al("PB", 512), al("PF", 64), al("PF", 64), al("PI", 64), al("PI", 64), al("PI", 8)
+    KSI, KSC, CLB, MK = al("PI", 128), al("PI", 128), al("PB", 128), al("PB", 128)
+    LRF, lr1, lr2, lr3, LRU = two("PF", 32), al("PF", 32), al("PF", 32), al("PF", 32), two("PU", 32)
+    KB, LG, WO = al("PB", 256), al("PB", 512), two("PF", 32)
+    HALT, GO, FRA, FR = al("PB", 32), al("PB", 32), al("PB", 32), two("PB", 32)
+    scn, HT, wy, SOFF = al("PF", 32), al("PF", 32), al("PF", 32), al("PU", 32)
+    vm, vq, vs, v37, vsum, vbp = (al("PI", 32) for _ in range(6))
+    VB16, VBL, VN, VNs, VC = al("PF", 64), al("PF", 32), two("PI", 32), al("PI", 32), two("PF", 32)
+    vd, vd2, KW, kw1 = al("PF", 32), al("PF", 32), al("PF", 32), al("PF", 32)
+    KJ, KM, NB, MN, UQ = al("PF", 128), al("PF", 128), al("PF", 8), al("PF", 8), al("PF", 8)
+    AB = [al("PF", 16 * q + 16) for q in range(8)]
+    KI, VW, VT = al("PI", 8), al("PI", 8), al("PF", 8)
+    mt, mo, to1, to2 = al("PF", 8), al("PF", 8), al("PF", 8), al("PF", 8)
+    MOFF, TOFF = two("PU", 8), two("PU", 8)
+    LI, L2, MG, MV = al("PI", 128), al("PI", 128), al("PB", 128), al("PB", 128)
+    ZI, ZJ, ZO, DNR = al("PI", 8), al("PI", 8), al("PU", 8), al("PB", 128)
+    HS, LS = two("PB", 128), two("PB", 128)
+    v1, a1, a2, VE = al("PF", 64), al("PF", 32), al("PF", 16), al("PF", 8)
+    DN, DNB, SENT, A16 = al("PF", 8), al("PB", 8), al("PB", 8), al("PF", 1)
+
+    def vbase(src):
+        copy(vs, src)
+        ts(vm, vs, 4095, ALU.bitwise_and)
+        tt(vq, vm, vm, ALU.mult)
+        ts(vsum, vq, 3, ALU.arith_shift_right)
+        ts(v37, vs, 37.0, ALU.mult)
+        tt(vsum, vsum, v37, ALU.add)
+        ts(vbp, vsum, 8191, ALU.bitwise_and)
+        ts(VBL, vbp, 16.0, ALU.mult)
+        v16ops(VB16, vbp)
+
+    def keys(v):
+        ts(kw1, v, 1024.0, ALU.mult)
+        tt(KW, kw1, LANE, ALU.add)
+        for i in range(16):
+            if i < CFG["kx"]: act(("KX", i, 512, 16), KW, AF.Copy, scale=m16(i))
+            else: ts(("KX", i, 512, 16), KW, m16(i), ALU.mult)
+        for k in range(4): mm([(("TPA", k * 128, k * 128 + 128), BOF, ("KX", k * 128, k * 128 + 128), True, True)], f32=True)
+        act(("KEYR", 0, 512), ("TPA", 0, 512), AF.Copy)
+
+    copy(VC[0], V0)
+    keys(V0)
+    vbase(VC[0])
+
+    for t in range(TS):
+        pr, nx, last = t % 2, (t + 1) % 2, t == TS - 1
+        partner = T.cores[rank ^ (1 + t % 7)]
+        cn, fr, vc = CN[pr], FR[pr], VC[pr]
+        zc = SD
+        for b in range(4):
+            p = b % 2
+            if b == 0: sq = SQ0
+            else:
+                sq = SQ[p]
+                o = sums(zc)
+                for m in range(2): act(sub(sq, m * 32, m * 32 + 32), o, AF.Square, BIAS[m])
+            tt(SI[p], sq, V16, ALU.add)
+            c = sub(cn, b * 64, b * 64 + 64)
+            ts(c, SI[p], 4, ALU.arith_shift_right, 8191, ALU.bitwise_and)
+            copy(C16[p], c)
+            zn = sub(ZH, b * 512, b * 512 + 512) if b < 3 else ZF
+            n = CFG["sp"]
+            for u in range(n):
+                c0, c1 = u * 32 // n, (u + 1) * 32 // n
+                yy, hu = sub(Y1[p], c0 * 16, c1 * 16), sub(HB[p], c0 * 16, c1 * 16)
+                gather("act", yy, XW, sub(C16[p], 32 + c0, 32 + c1))
+                o16 = sub(C16[p], c0, c1)
+                op("dve", lambda o16=o16, yy=yy, hu=hu: g.vector.tensor_tensor(out=ap(hu), in0=ind(XW, o16), in1=ap(yy), op=ALU.max),
+                   [XW, o16, yy], [hu], gat(512 // n))
+            for h in range(2):
+                dps, zs = ("D%d" % h, 0, 256), sub(zc, h * 256, h * 256 + 256)
+                mm([(dps, NID, zs, True, False)])
+                mm([(dps, ID, sub(HB[p], h * 256, h * 256 + 256), False, True)])
+                act(sub(zn, h * 256, h * 256 + 256), dps, AF.Abs)
+            zc = zn
+        if t:
+            for k in range(8): pass
+            mm([(("TPB", k * 32, k * 32 + 32), ID, fr, True, True) for k in range(8)])
+            tt(tda, TM[nx] if t > 1 else CN[0], cn, ALU.subtract)
+            tt(tdb, ("TPB", 0, 256), tda, ALU.mult)
+            tt(("YT", 0, 256) if last else TM[pr], tdb, cn, ALU.add)
+        for h in range(2): ts(sub(GE, h * 256, h * 256 + 256), sub(zc, h * 256, h * 256 + 256), sub(TH, t, t + 1), ALU.is_ge)
+        o = sums(GE, fr if t else None)
+        ts(HALT, o, 8.5, ALU.is_ge)
+        p2, p12 = ("HP", 0, 32), ("HP", 32, 64)
+        mm([(p2, BO, HALT, True, True), (p12, TRI, HALT, True, True)])
+        tt(HT, HALT, TL, ALU.mult)
+        op("dve", lambda p2=p2: g.vector.tensor_tensor_scan(out=ap(scn), data0=ap(P16N), data1=ap(p2), initial=ap(INI), op0=ALU.add, op1=ALU.add),
+           [P16N, p2, INI], [scn], dv(32))
+        tt(wy, p12, HT, ALU.subtract)
+        tt(WO[pr], wy, scn, ALU.add)
+        copy(SOFF, WO[pr])
+        scatter(("KSD%d" % t, 0, 1536), SOFF, ("KEYR", 0, 512))
+        ks = ("KSD%d" % t, 0, 128)
+        send(partner, ("KL", t * 128, t * 128 + 128), ks, "rk%d" % t, 2.4)
+        kws = ("KWS", t * 8, t * 8 + 8)
+        tt(KM, ks, DM, ALU.mult)
+        for q in range(8):
+            if q < CFG["kw"]: act(sub(KJ, q * 16, q * 16 + 16), sub(KM, q * 16, q * 16 + 16), AF.Copy, acc_o=sub(kws, q, q + 1))
+            else: red(sub(kws, q, q + 1), sub(KM, q * 16, q * 16 + 16), ALU.add)
+        send(partner, ("KWL", t * 8, t * 8 + 8), kws, "rw%d" % t, 1.8)
+        ts(GO, WO[pr], 127.5, ALU.is_lt)
+        if t:
+            tt(FRA, fr, GO, ALU.add)
+            tt(lr1, WO[pr], LRF[nx], ALU.subtract)
+            ts(lr2, lr1, 128.0 * t, ALU.add)
+            tt(lr3, lr2, GO, ALU.mult)
+            tt(LRF[pr], LRF[nx], lr3, ALU.add)
+        else:
+            copy(FRA, GO)
+            tt(LRF[pr], WO[pr], GO, ALU.mult)
+        copy(LRU[pr], LRF[pr])
+        copy(ZI, kws)
+        ts(ZJ, ZI, 511, ALU.bitwise_and)
+        copy(ZO, ZJ)
+        for b in range(4):
+            gather("act", sub(ZG, b * 128, b * 128 + 128), SD if b == 0 else sub(ZH, b * 512 - 512, b * 512), ZO)
+        us = ("BD", 0, 32)
+        mm([(us, sel(i), sub(ZG, i, 512, 16), i == 0, i == 15) for i in range(16)])
+        for m in range(2): act(sub(SQS, m * 32, m * 32 + 32), us, AF.Square, BIAS[m])
+        ts(VSW, ZI, 10, ALU.arith_shift_right, 8191, ALU.bitwise_and)
+        ts(sub(VSE, 0, 8), VSW, 16.0, ALU.mult, -64.0 * KS[0] ** 2, ALU.add)
+        copy(sub(VSE, 8, 16), sub(VSE, 0, 8))
+        copy(sub(VSE, 16, 32), sub(VSE, 0, 16))
+        ts(sub(VSE, 32, 64), sub(VSE, 0, 32), 64.0 * (KS[0] ** 2 - KS[1] ** 2), ALU.add)
+        tt(SIS, SQS, VSE, ALU.add)
+        ts(CS, SIS, 4, ALU.arith_shift_right, 8191, ALU.bitwise_and)
+        copy(sub(OFF, t * 64, t * 64 + 64), CS)
+        copy(KSI, ks)
+        ts(KSC, KSI, 7, ALU.arith_shift_right, 7, ALU.bitwise_and)
+        ts(CLB, KSC, 1.0, ALU.add)
+        mm([(("BD", 64, 128), CLB, RHE, True, True)])
+        copy(sub(CLX, t * 64, t * 64 + 64), ("BD", 64, 128))
+        if not last:
+            gather("act", ("ZS", t * 128, t * 128 + 128), ZF, ZO)
+            send(partner, ("ZL", t * 128, t * 128 + 128), ("ZS", t * 128, t * 128 + 128), "rz%d" % t, 2.2)
+        kl, kwl = ("KL", t * 128, t * 128 + 128), ("KWL", t * 8, t * 8 + 8)
+        ts(NB, kwl, -1.0, ALU.mult, 256.0, ALU.add)
+        for q in range(8): act(AB[q], sub(kl, 0, 16 * q + 16), AF.Abs, sub(NB, q, q + 1))
+        copy(KI, kwl)
+        ts(VW, KI, 10, ALU.arith_shift_right)
+        tt(VT, VW, TRW, ALU.subtract)
+        copy(LI, kl)
+        ts(L2, LI, 7, ALU.arith_shift_right, 7, ALU.bitwise_and)
+        ts(MG, L2, 1.0, ALU.add, m16(2), ALU.mult)
+        tt(MV, MG, SC, ALU.add)
+        ts(SENT, kwl, float(W * 1024), ALU.is_ge)
+        for q in range(8): red(sub(MN, q, q + 1), AB[q], ALU.min)
+        ts(UQ, MN, 255.5, ALU.is_ge)
+        tt(mt, UQ, VT, ALU.mult)
+        tt(mo, mt, TRW, ALU.add)
+        copy(MOFF[pr], mo)
+        scatter(MAP, MOFF[pr], MV)
+        tiles = 8 * (t + 1)
+        for k in range((t + 2) // 2):
+            bank = ("TPA", "TPB")[k]
+            nt = min(16, tiles - 16 * k)
+            for j in range(nt // 2):
+                jj = k * 8 + j
+                gather("dve" if jj in CFG["map"][t] else "act", ("G", jj * 256, jj * 256 + 256), MAP, sub(OFF, jj * 16, jj * 16 + 16))
+                mm([((bank, (2 * j + w) * 24, (2 * j + w) * 24 + 24), ("G", jj * 256 + w * 128, jj * 256 + w * 128 + 128), RK, True, True) for w in range(2)])
+            nc = nt * 8
+            hs, ls, mk = sub(HS[k], 0, nc), sub(LS[k], 0, nc), sub(MK, 0, nc)
+            tt(mk, (bank, 2, nt * 24, 3), sub(CLX, k * 128, k * 128 + nc), ALU.is_ge)
+            copy(hs, (bank, 0, nt * 24, 3))
+            tt(ls, (bank, 1, nt * 24, 3), mk, ALU.mult)
+            for d in range(8):
+                ts(("HI", k * 1024 + d, k * 1024 + nc * 8, 8), hs, float(d + 1), ALU.is_equal)
+            for d in range(16):
+                ts(("LO", k * 2048 + d, k * 2048 + nc * 16, 16), ls, float(d + 1), ALU.is_equal)
+            mm([(("HP", 0, 64), ("LO", k * 2048 + u * 128, k * 2048 + u * 128 + 128), ("HI", k * 1024 + u * 64, k * 1024 + u * 64 + 64),
+                 k == 0 and u == 0, 16 * k + u == tiles - 1) for u in range(nt)])
+        tt(v1, ("HP", 0, 64), DG, ALU.mult)
+        tt(a1, sub(v1, 0, 32), sub(v1, 32, 64), ALU.add)
+        tt(a2, sub(a1, 0, 16), sub(a1, 16, 32), ALU.add)
+        tt(VE, sub(a2, 0, 8), sub(a2, 8, 16), ALU.add)
+        tt(DN, VE, UQ, ALU.is_lt)
+        tt(DNB, VE, UQ, ALU.is_lt)
+        aps = ("HP", 0, 8)
+        mm([(aps, N16, SENT, True, False), (aps, P16, DNB, False, True)])
+        red(A16, aps, ALU.add)
+        if not last: ts(V16, VB16, A16, ALU.add)
+        tt(to1, DN, VT, ALU.mult)
+        tt(to2, to1, TRW, ALU.add)
+        copy(TOFF[pr], to2)
+        if not last: scatter(("X", 0, NM), TOFF[pr], ("ZL", t * 128, t * 128 + 128))
+        mm([(("BD", i, 128, 16), ("EI", i * 128, i * 128 + 128), DNB, True, True) for i in range(16)])
+        copy(DNR, ("BD", 0, 128))
+        nds = ("NDS", t * 128, t * 128 + 128)
+        ts(nds, ("BD", 0, 128), -1.0, ALU.mult, 1.0, ALU.add)
+        scatter(MAP, MOFF[pr], DNR)
+        ndl = ("NDL", t * 128, t * 128 + 128)
+        send(partner, ndl, nds, "rb%d" % t, 2.0)
+        vn = VN[pr]
+        ts(VNs, VBL, A16, ALU.add)
+        ts(vn, VNs, 4, ALU.arith_shift_right, 8191, ALU.bitwise_and)
+        if not last: keys(vn)
+        krep = []
+        for b in range(t + 1):
+            for j in range(b * 4, b * 4 + 4):
+                gather("dve" if j in CFG["hg"][t] else "act", ("HG", j * 256, j * 256 + 256), MAP, sub(OFF, j * 16, j * 16 + 16))
+            tl = [("HG", b * 1024 + k * 128, b * 1024 + k * 128 + 128) for k in range(8)] + ([ndl] if b == t else [])
+            kp, kb = ("BD", b * 64, b * 64 + 64), sub(KB, b * 64, b * 64 + 64)
+            mm([(kp, x, RHE, n == 0, n == len(tl) - 1) for n, x in enumerate(tl)])
+            ts(kb, kp, 0.5, ALU.is_gt, 8.0, ALU.mult)
+            if not last: tt(sub(CLX, b * 64, b * 64 + 64), sub(CLX, b * 64, b * 64 + 64), kb, ALU.max)
+            krep.append((("TPB", b * 128, b * 128 + 128), sub(kb, 0, 8), ID, True, True))
+        if not last: scatter(MAP, MOFF[pr], ZERO)
+        mm(krep, p8=True)
+        e = 128 * t + 128
+        op("act", lambda e=e: g.scalar.activation(out=T.PB[0:8, KT[1]:KT[1] + e], in_=T.TPB[0:8, 0:e], func=AF.Copy), [("TPB", 0, e)], [sub(KT, 0, e)], dv(e))
+        op("pe", lambda e=e: g.tensor.matmul(T.TPB[:, 0:e], T.PB[0:8, EXP[1]:EXP[2]], T.PB[0:8, KT[1]:KT[1] + e], True, True),
+           [EXP, sub(KT, 0, e)], [("TPB", 0, e)], e * PEC)
+        act(sub(KRP, 0, e), ("TPB", 0, e), AF.Copy)
+        for h in range(2): gather("dve" if CFG["lg"] == h else "act", sub(LG, h * 256, h * 256 + 256), KRP, sub(LRU[pr], h * 16, h * 16 + 16))
+        bw = ("BD", 384, 416)
+        mm([(bw, sel(i), sub(LG, i, 512, 16), i == 0, i == 15) for i in range(16)])
+        frn = FR[nx]
+        tt(frn, FRA, bw, ALU.is_gt)
+        vcn = ("YS", 0, 32) if last else VC[nx]
+        tt(vd, vc, vn, ALU.subtract)
+        tt(vd2, vd, frn, ALU.mult)
+        tt(vcn, vd2, vn, ALU.add)
+        if not last: vbase(vcn)
+
+    dma(T.yt[:], T.YT[:], [("YT", 0, 256)], [], "st_t", 2.0)
+    copy(("YS", 32, 64), FR[TS % 2])
+    dma(T.ys[:], T.YS[:], [("YS", 0, 64)], [], "st_s", 2.0)
+
+    n = len(ops)
+    if n not in ORDER:
+        users = [[] for _ in range(n)]
+        for i, o in enumerate(ops):
+            for d in o["deps"]: users[d].append(i)
+        pri = [0.0] * n
+        for i in range(n - 1, -1, -1):
+            best = 0.0
+            for u in users[i]: best = max(best, pri[u] + (HOP if ops[u]["deps"][i] else 0.0))
+            pri[i] = best + ops[i]["dur"] + ops[i]["lat"]
+            if ops[i]["early"]: pri[i] = 400.0 + pri[i] * 0.01
+        busy = {}
+        start = [0.0] * n
+        left = [len(o["deps"]) for o in ops]
+        ready = [i for i in range(n) if left[i] == 0]
+        while ready:
+            i = max(ready, key=lambda j: (pri[j], -j))
+            ready.remove(i)
+            o = ops[i]
+            at = 0.0
+            for d, w in o["deps"].items():
+                e = start[d] + ops[d]["dur"]
+                at = max(at, e + ops[d]["lat"] + HOP if w else e)
+            if o["eng"] != "net":
+                sl = busy.setdefault(o["eng"], [])
+                k = len(sl)
+                while k > 0 and sl[k - 1][1] > at: k -= 1
+                while k < len(sl) and sl[k][0] < at + o["dur"] - 1e-9:
+                    at = max(at, sl[k][1])
+                    k += 1
+                sl.insert(k, (at, at + o["dur"]))
+            start[i] = at
+            CFG["span"][0] = max(CFG["span"][0], at + o["dur"] + o["lat"])
+            for u in users[i]:
+                left[u] -= 1
+                if left[u] == 0: ready.append(u)
+        ORDER[n] = sorted(range(n), key=lambda i: (start[i], i))
+    order = ORDER[n]
+
+    pos, cnt = {}, {}
+    for i in order:
+        q = ops[i]["eng"]
+        cnt[q] = cnt.get(q, 0) + 1
+        pos[i] = cnt[q]
+    known, vcs, waits, needed, final = {}, {}, {}, set(), {}
+    for i in order:
+        o = ops[i]
+        q = o["eng"]
+        final[q] = i
+        if q == "net":
+            vcs[i] = {("ev", i): 1}
+            continue
+        kn = known.setdefault(q, {})
+        mine = []
+        for d in sorted((d for d, w in o["deps"].items() if w), key=lambda d: -pos[d]):
+            key, val = (("ev", d), 1) if ops[d]["event"] else (ops[d]["eng"], pos[d])
+            if kn.get(key, 0) >= val: continue
+            mine.append(d)
+            needed.add(d)
+            for k2, x2 in vcs[d].items():
+                if kn.get(k2, 0) < x2: kn[k2] = x2
+        waits[i] = mine
+        v = dict(kn)
+        v[("ev", i) if o["event"] else q] = 1 if o["event"] else pos[i]
+        vcs[i] = v
+    for q in ("pe", "dve", "act"): needed.add(final[q])
+
+    eng = {"pe": g.tensor, "dve": g.vector, "act": g.scalar, "gp": g, "sp": g.sync}
+    num, tot = {}, {}
+    for i in order:
+        q = ops[i]["eng"]
+        if i in needed and not ops[i]["event"]:
+            tot[q] = tot.get(q, 0) + 1
+            num[i] = tot[q]
+    for i in order:
+        o = ops[i]
+        q = o["eng"]
+        if q == "net": continue
+        best = {}
+        for d in waits[i]:
+            s, v = ops[d]["event"] if ops[d]["event"] else ("c_" + ops[d]["eng"], num[d])
+            best[s] = max(best.get(s, 0), v)
+        for s in best: eng[q].wait_ge(T.sem[s], best[s])
+        x = o["fn"]()
+        if i in num: x.then_inc(T.sem["c_" + q], 1)
+    for q in tot: g.sync.wait_ge(T.sem["c_" + q], tot[q])
+    g.sync.wait_ge(T.sem.lsem, used[0])
+    for s in ("st_t", "st_s"): g.sync.wait_ge(T.sem[s], 16)

@@ -2,7 +2,7 @@ from concourse.mybir import AluOpType as ALU, AxisListType, ActivationFunctionTy
 
 W, L, TS = 8192, 512, 4
 KS = (3, 29)
-NM = 8320
+NM = 16384 + 256
 
 SCRATCH = {
     "X": ("sbuf", [128, NM], "bfloat16"), "MAP": ("sbuf", [128, NM], "bfloat16"),
@@ -11,6 +11,7 @@ SCRATCH = {
     "KL": ("sbuf", [128, 512], "float32"), "KWS": ("sbuf", [128, 32], "float32"), "KWL": ("sbuf", [128, 32], "float32"),
     "ZS": ("sbuf", [128, 384], "bfloat16"), "ZL": ("sbuf", [128, 384], "bfloat16"),
     "NDS": ("sbuf", [128, 512], "bfloat16"), "NDL": ("sbuf", [128, 512], "bfloat16"),
+    "MVS": ("sbuf", [128, 512], "bfloat16"), "MVL": ("sbuf", [128, 512], "bfloat16"),
     "G": ("sbuf", [128, 4096], "bfloat16"), "HG": ("sbuf", [128, 4096], "bfloat16"),
     "LO": ("sbuf", [128, 4096], "bfloat16"), "HI": ("sbuf", [128, 2048], "bfloat16"),
     "KX": ("sbuf", [128, 512], "float32"), "KEYR": ("sbuf", [128, 512], "float32"),
@@ -19,17 +20,18 @@ SCRATCH = {
     "PU": ("sbuf", [128, 1000], "uint16"), "PB": ("sbuf", [128, 12000], "bfloat16"),
 }
 for _t in range(TS): SCRATCH["KSD%d" % _t] = ("sbuf", [128, 1536], "float32")
-PSUM = ("U0", "D0", "D1", "TPA", "TPB", "HP", "BD")
+PSUM = ("U0", "D0", "D1", "D2", "TPA", "TPB", "HP", "BD")
 for _b in PSUM: SCRATCH[_b] = ("psum", [128, 512], "float32")
 QUEUES = ("pe", "dve", "act", "gp")
 SEMAPHORES = (["c_" + q for q in QUEUES] + ["ld_x", "ld_sd", "ld_v", "ld_th", "st_t", "st_s", "lsem"]
-              + ["%s%d" % (k, t) for k in ("rk", "rw", "rz", "rb") for t in range(TS)])
+              + ["%s%d" % (k, t) for k in ("rk", "rw", "rm", "rz", "rb") for t in range(TS)])
 
-CYC, PEC, HOP = 0.001, 0.00086, 0.1
+CYC, PEC, HOP = 0.001, 0.00086, 0.16
 ORDER = {}
-CFG = {"map": ((1, 2), (1, 3, 4, 7), (1, 3, 4, 10), (1, 3, 9, 10, 12, 14)),
-       "hg": ((0, 3), (1, 2, 4, 5), (2, 3, 4, 5, 7, 9, 11), (0, 2, 4, 6, 10, 11, 13, 14)),
-       "sp": 4, "kw": 3, "kx": 16, "lg": 1, "span": [0.0]}
+CFG = {"map": ((1, 2), (1, 2, 4, 6), (2, 4, 5, 6, 8), (3, 5, 6, 7, 11, 13)),
+       "hg": ((0, 1, 2, 3), (2, 3, 4, 5), (0, 3, 8, 9, 11), (0, 3, 4, 7, 8, 11, 13, 14)),
+       "cut": ((0, 8), (8, 16), (16, 24), (24, 32)), "dcut": ((0, 16), (16, 24), (24, 32)),
+       "kw": 3, "kx": 8, "lg": 0, "span": [0.0]}
 
 
 def dv(n, c=1.0):
@@ -70,7 +72,7 @@ def rank_program(g, core, T, topo):
             ex = b in PSUM
             for (l2, h2, m, wr) in acc.get(b, []):
                 if l2 < hi and lo < h2 or ex:
-                    need(m, ops[m]["eng"] != eng or eng in ("sp", "net"))
+                    need(m, ops[m]["eng"] != eng or eng in ("sp", "net") or not (wr or ex))
         for m in after: need(m, False)
         ops.append({"eng": eng, "fn": fn, "deps": deps, "dur": dur, "event": event, "lat": lat, "early": early})
         for (b, lo, hi) in reads:
@@ -124,7 +126,7 @@ def rank_program(g, core, T, topo):
         op("dve", fn, rd, [rg(o)], dv(wd(o), fastc(o, a)))
 
     def fill(o, v):
-        op("dve", lambda: g.vector.memset(ap(o), v), [], [rg(o)], dv(wd(o), fastc(o)), early=128 < wd(o) < 8000)
+        op("dve", lambda: g.vector.memset(ap(o), v), [], [rg(o)], dv(wd(o), fastc(o)), early=128 < wd(o))
 
     def red(o, a, f):
         op("dve", lambda: g.vector.tensor_reduce(out=ap(o), in_=ap(a), axis=AxisListType.X, op=f), [rg(a)], [rg(o)], dv(wd(a)))
@@ -186,14 +188,14 @@ def rank_program(g, core, T, topo):
         s = op("gp", fn, [rg(i)], [], 0.1)
         op("net", None, [], [rg(o)], 0.0, event=(sem, len(en)), after=(s,), lat=lat)
 
-    def dma(o_ap, i_ap, rd, wr, sem, lat):
-        op("sp", lambda: g.sync.dma_start(o_ap, i_ap).then_inc(T.sem[sem], 16), rd, wr, 0.1, event=(sem, 16), lat=lat)
+    def dma(o_ap, i_ap, rd, wr, sem, lat, eng="sp"):
+        op(eng, lambda: (g.sync if eng == "sp" else g.scalar).dma_start(o_ap, i_ap).then_inc(T.sem[sem], 16), rd, wr, 0.1, event=(sem, 16), lat=lat)
 
     V0, THI, SD, XW = ("V0", 0, 32), ("THI", 0, 4), ("SD", 0, 512), ("X", 0, W)
-    dma(T.V0[:], T.v0[:], [], [V0], "ld_v", 2.0)
+    dma(T.V0[:], T.v0[:], [], [V0], "ld_v", 2.0, "act")
+    dma(T.THI[:], T.th[:], [], [THI], "ld_th", 3.0, "act")
     dma(T.SD[:], T.sd[:], [], [SD], "ld_sd", 2.5)
     dma(T.X[:, 0:W], T.x[:], [], [XW], "ld_x", 10.0)
-    dma(T.THI[:], T.th[:], [], [THI], "ld_th", 3.0)
 
     ONE, BO, t0, ID = al("PB", 128), al("PB", 128), al("PB", 128), al("PB", 128)
     fill(ONE, 1.0)
@@ -243,10 +245,12 @@ def rank_program(g, core, T, topo):
     o = sums(SD)
     for m in range(2): act(sub(SQ0, m * 32, m * 32 + 32), o, AF.Square, BIAS[m])
 
-    MAP = ("MAP", 0, NM)
-    fill(MAP, 0.0)
+    MAP, MAPW = ("MAP", 0, NM), ("MAP", 0, W)
+    fill(MAPW, 0.0)
     TH = al("PF", 4)
     copy(TH, THI)
+    NEG = al("PF", 1)
+    fill(NEG, -1.0)
     TRI, nbo, BOF = al("PB", 128), al("PB", 128), al("PF", 128)
     ts(nbo, BO, -1.0, ALU.mult)
     asel(TRI, nbo, [[-1, 128]], ALU.is_ge, 0, 1)
@@ -258,11 +262,22 @@ def rank_program(g, core, T, topo):
     ex0, EXP, KT = al("PB", 128), al("PB", 128), al("PB", 512)
     asel(ex0, ONE, [[1, 128]], ALU.is_ge, 0, -16)
     asel(EXP, ex0, [[-1, 128]], ALU.is_ge, 15, 16)
-    DM, DG = al("PF", 128), al("PF", 64)
-    for k in range(8): copy(sub(DM, k * 16, k * 16 + 16), M16)
-    copy(DG, sub(BO, 0, 128, 2))
+    DM, dm1, dm2 = al("PF", 128), al("PF", 16), al("PF", 16)
+    ts(dm1, M16, 33554432.0, ALU.mult, -17.0, ALU.add)
+    ts(sub(dm2, 1, 16), sub(M16, 0, 15), -1.0, ALU.mult)
+    ts(sub(dm2, 0, 1), m16(15), -1.0, ALU.mult)
+    for k in range(8): tt(sub(DM, k * 16, k * 16 + 16), dm1, dm2, ALU.add)
+    pc, c8, c9, g8, g9, dl = (al("PF", 1) for _ in range(6))
+    DL = al("PU", 1)
+    iota(pc, [[0, 1]], 0, 1)
+    tt(g8, pc, IC, ALU.subtract)
+    ts(c8, IC, 7.5, ALU.is_ge, -8.0, ALU.mult)
+    tt(c9, c8, IC, ALU.add)
+    ts(g9, g8, 0.5, ALU.mult)
+    tt(dl, g9, c9, ALU.add)
+    copy(DL, dl)
     i8, TRW, SROW = al("PF", 8), al("PF", 8), al("PF", 128)
-    iota(i8, [[16, 8]], W, 0)
+    iota(i8, [[16, 8]], 2 * W + 128, 0)
     ts(TRW, i8, IC, ALU.add)
     iota(SROW, [[1024, 128]], W * 1024 + 896, 0)
     for t in range(TS): copy(("KSD%d" % t, 0, 128), SROW)
@@ -290,18 +305,19 @@ def rank_program(g, core, T, topo):
     HALT, GO, FRA, FR = al("PB", 32), al("PB", 32), al("PB", 32), two("PB", 32)
     scn, HT, wy, SOFF = al("PF", 32), al("PF", 32), al("PF", 32), al("PU", 32)
     vm, vq, vs, v37, vsum, vbp = (al("PI", 32) for _ in range(6))
+    SV0, SIN = al("PF", 64), al("PI", 64)
     VB16, VBL, VN, VNs, VC = al("PF", 64), al("PF", 32), two("PI", 32), al("PI", 32), two("PF", 32)
     vd, vd2, KW, kw1 = al("PF", 32), al("PF", 32), al("PF", 32), al("PF", 32)
-    KJ, KM, NB, MN, UQ = al("PF", 128), al("PF", 128), al("PF", 8), al("PF", 8), al("PF", 8)
+    KJ, KM, MN, UQ = al("PF", 128), al("PF", 128), al("PF", 8), al("PF", 16)
+    fill(UQ, 0.0)
     AB = [al("PF", 16 * q + 16) for q in range(8)]
     KI, VW, VT = al("PI", 8), al("PI", 8), al("PF", 8)
-    mt, mo, to1, to2 = al("PF", 8), al("PF", 8), al("PF", 8), al("PF", 8)
+    mt, mo, to1, to2 = al("PF", 8), al("PF", 8), al("PF", 16), al("PF", 8)
     MOFF, TOFF = two("PU", 8), two("PU", 8)
-    LI, L2, MG, MV = al("PI", 128), al("PI", 128), al("PB", 128), al("PB", 128)
+    MG = al("PB", 128)
     ZI, ZJ, ZO, DNR = al("PI", 8), al("PI", 8), al("PU", 8), al("PB", 128)
     HS, LS = two("PB", 128), two("PB", 128)
-    v1, a1, a2, VE = al("PF", 64), al("PF", 32), al("PF", 16), al("PF", 8)
-    DN, DNB, SENT, A16 = al("PF", 8), al("PB", 8), al("PB", 8), al("PF", 1)
+    HPS, DNB, SENT, A16 = al("PF", 64), al("PB", 16), al("PB", 8), al("PF", 1)
 
     def vbase(src):
         copy(vs, src)
@@ -313,6 +329,7 @@ def rank_program(g, core, T, topo):
         ts(vbp, vsum, 8191, ALU.bitwise_and)
         ts(VBL, vbp, 16.0, ALU.mult)
         v16ops(VB16, vbp)
+        tt(SV0, SQ0, VB16, ALU.add)
 
     def keys(v):
         ts(kw1, v, 1024.0, ALU.mult)
@@ -338,33 +355,34 @@ def rank_program(g, core, T, topo):
             else:
                 sq = SQ[p]
                 o = sums(zc)
-                for m in range(2): act(sub(sq, m * 32, m * 32 + 32), o, AF.Square, BIAS[m])
-            tt(SI[p], sq, V16, ALU.add)
-            c = sub(cn, b * 64, b * 64 + 64)
-            ts(c, SI[p], 4, ALU.arith_shift_right, 8191, ALU.bitwise_and)
-            copy(C16[p], c)
+                for m in (1, 0): act(sub(sq, m * 32, m * 32 + 32), o, AF.Square, BIAS[m])
+            c16 = C16[p]
+            for m in (1, 0):
+                k0, k1 = m * 32, m * 32 + 32
+                if b or not t: tt(sub(SI[p], k0, k1), sub(sq, k0, k1), sub(V16, k0, k1), ALU.add)
+                c = sub(cn, b * 64 + k0, b * 64 + k1)
+                ts(c, sub(SI[p] if b or not t else SIN, k0, k1), 4, ALU.arith_shift_right, 8191, ALU.bitwise_and)
+                copy(sub(c16, k0, k1), c)
             zn = sub(ZH, b * 512, b * 512 + 512) if b < 3 else ZF
-            n = CFG["sp"]
-            for u in range(n):
-                c0, c1 = u * 32 // n, (u + 1) * 32 // n
+            for c0, c1 in CFG["cut"]:
                 yy, hu = sub(Y1[p], c0 * 16, c1 * 16), sub(HB[p], c0 * 16, c1 * 16)
-                gather("act", yy, XW, sub(C16[p], 32 + c0, 32 + c1))
-                o16 = sub(C16[p], c0, c1)
+                gather("act", yy, XW, sub(c16, 32 + c0, 32 + c1))
+                o16 = sub(c16, c0, c1)
                 op("dve", lambda o16=o16, yy=yy, hu=hu: g.vector.tensor_tensor(out=ap(hu), in0=ind(XW, o16), in1=ap(yy), op=ALU.max),
-                   [XW, o16, yy], [hu], gat(512 // n))
-            for h in range(2):
-                dps, zs = ("D%d" % h, 0, 256), sub(zc, h * 256, h * 256 + 256)
-                mm([(dps, NID, zs, True, False)])
-                mm([(dps, ID, sub(HB[p], h * 256, h * 256 + 256), False, True)])
-                act(sub(zn, h * 256, h * 256 + 256), dps, AF.Abs)
+                   [XW, o16, yy], [hu], gat(c1 * 16 - c0 * 16))
+            for h, (c0, c1) in enumerate(CFG["dcut"]):
+                r0, r1 = c0 * 16, c1 * 16
+                dps = ("D%d" % h, 0, r1 - r0)
+                mm([(dps, NID, sub(zc, r0, r1), True, False)])
+                mm([(dps, ID, sub(HB[p], r0, r1), False, True)])
+                act(sub(zn, r0, r1), dps, AF.Abs)
             zc = zn
         if t:
-            for k in range(8): pass
             mm([(("TPB", k * 32, k * 32 + 32), ID, fr, True, True) for k in range(8)])
             tt(tda, TM[nx] if t > 1 else CN[0], cn, ALU.subtract)
             tt(tdb, ("TPB", 0, 256), tda, ALU.mult)
             tt(("YT", 0, 256) if last else TM[pr], tdb, cn, ALU.add)
-        for h in range(2): ts(sub(GE, h * 256, h * 256 + 256), sub(zc, h * 256, h * 256 + 256), sub(TH, t, t + 1), ALU.is_ge)
+        for c0, c1 in CFG["dcut"]: ts(sub(GE, c0 * 16, c1 * 16), sub(zc, c0 * 16, c1 * 16), sub(TH, t, t + 1), ALU.is_ge)
         o = sums(GE, fr if t else None)
         ts(HALT, o, 8.5, ALU.is_ge)
         p2, p12 = ("HP", 0, 32), ("HP", 32, 64)
@@ -379,11 +397,17 @@ def rank_program(g, core, T, topo):
         ks = ("KSD%d" % t, 0, 128)
         send(partner, ("KL", t * 128, t * 128 + 128), ks, "rk%d" % t, 2.4)
         kws = ("KWS", t * 8, t * 8 + 8)
-        tt(KM, ks, DM, ALU.mult)
+        tt(KM, ks, DM, ALU.min)
         for q in range(8):
             if q < CFG["kw"]: act(sub(KJ, q * 16, q * 16 + 16), sub(KM, q * 16, q * 16 + 16), AF.Copy, acc_o=sub(kws, q, q + 1))
             else: red(sub(kws, q, q + 1), sub(KM, q * 16, q * 16 + 16), ALU.add)
         send(partner, ("KWL", t * 8, t * 8 + 8), kws, "rw%d" % t, 1.8)
+        copy(KSI, ks)
+        ts(KSC, KSI, 7, ALU.arith_shift_right, 7, ALU.bitwise_and)
+        mvs = ("MVS", t * 128, t * 128 + 128)
+        ts(MG, KSC, 1.0, ALU.add, m16(2), ALU.mult)
+        tt(mvs, MG, SC, ALU.add)
+        send(partner, ("MVL", t * 128, t * 128 + 128), mvs, "rm%d" % t, 2.2)
         ts(GO, WO[pr], 127.5, ALU.is_lt)
         if t:
             tt(FRA, fr, GO, ALU.add)
@@ -395,7 +419,7 @@ def rank_program(g, core, T, topo):
             copy(FRA, GO)
             tt(LRF[pr], WO[pr], GO, ALU.mult)
         copy(LRU[pr], LRF[pr])
-        copy(ZI, kws)
+        ts(ZI, kws, 256.0, ALU.add)
         ts(ZJ, ZI, 511, ALU.bitwise_and)
         copy(ZO, ZJ)
         for b in range(4):
@@ -411,8 +435,6 @@ def rank_program(g, core, T, topo):
         tt(SIS, SQS, VSE, ALU.add)
         ts(CS, SIS, 4, ALU.arith_shift_right, 8191, ALU.bitwise_and)
         copy(sub(OFF, t * 64, t * 64 + 64), CS)
-        copy(KSI, ks)
-        ts(KSC, KSI, 7, ALU.arith_shift_right, 7, ALU.bitwise_and)
         ts(CLB, KSC, 1.0, ALU.add)
         mm([(("BD", 64, 128), CLB, RHE, True, True)])
         copy(sub(CLX, t * 64, t * 64 + 64), ("BD", 64, 128))
@@ -420,56 +442,51 @@ def rank_program(g, core, T, topo):
             gather("act", ("ZS", t * 128, t * 128 + 128), ZF, ZO)
             send(partner, ("ZL", t * 128, t * 128 + 128), ("ZS", t * 128, t * 128 + 128), "rz%d" % t, 2.2)
         kl, kwl = ("KL", t * 128, t * 128 + 128), ("KWL", t * 8, t * 8 + 8)
-        ts(NB, kwl, -1.0, ALU.mult, 256.0, ALU.add)
-        for q in range(8): act(AB[q], sub(kl, 0, 16 * q + 16), AF.Abs, sub(NB, q, q + 1))
-        copy(KI, kwl)
+        for q in range(8): act(AB[q], sub(kl, 0, 16 * q + 16), AF.Abs, sub(kwl, q, q + 1), NEG)
+        ts(KI, kwl, 256.0, ALU.add)
         ts(VW, KI, 10, ALU.arith_shift_right)
         tt(VT, VW, TRW, ALU.subtract)
-        copy(LI, kl)
-        ts(L2, LI, 7, ALU.arith_shift_right, 7, ALU.bitwise_and)
-        ts(MG, L2, 1.0, ALU.add, m16(2), ALU.mult)
-        tt(MV, MG, SC, ALU.add)
         ts(SENT, kwl, float(W * 1024), ALU.is_ge)
         for q in range(8): red(sub(MN, q, q + 1), AB[q], ALU.min)
-        ts(UQ, MN, 255.5, ALU.is_ge)
-        tt(mt, UQ, VT, ALU.mult)
+        uq = sub(UQ, 0, 8)
+        ts(uq, MN, 255.5, ALU.is_ge)
+        tt(mt, uq, VT, ALU.mult)
         tt(mo, mt, TRW, ALU.add)
         copy(MOFF[pr], mo)
-        scatter(MAP, MOFF[pr], MV)
+        scatter(MAP, MOFF[pr], ("MVL", t * 128, t * 128 + 128))
         tiles = 8 * (t + 1)
         for k in range((t + 2) // 2):
             bank = ("TPA", "TPB")[k]
             nt = min(16, tiles - 16 * k)
             for j in range(nt // 2):
                 jj = k * 8 + j
-                gather("dve" if jj in CFG["map"][t] else "act", ("G", jj * 256, jj * 256 + 256), MAP, sub(OFF, jj * 16, jj * 16 + 16))
+                gather("dve" if jj in CFG["map"][t] else "act", ("G", jj * 256, jj * 256 + 256), MAPW, sub(OFF, jj * 16, jj * 16 + 16))
                 mm([((bank, (2 * j + w) * 24, (2 * j + w) * 24 + 24), ("G", jj * 256 + w * 128, jj * 256 + w * 128 + 128), RK, True, True) for w in range(2)])
             nc = nt * 8
             hs, ls, mk = sub(HS[k], 0, nc), sub(LS[k], 0, nc), sub(MK, 0, nc)
+            copy(ls, (bank, 1, nt * 24, 3))
             tt(mk, (bank, 2, nt * 24, 3), sub(CLX, k * 128, k * 128 + nc), ALU.is_ge)
-            copy(hs, (bank, 0, nt * 24, 3))
-            tt(ls, (bank, 1, nt * 24, 3), mk, ALU.mult)
-            for d in range(8):
-                ts(("HI", k * 1024 + d, k * 1024 + nc * 8, 8), hs, float(d + 1), ALU.is_equal)
             for d in range(16):
                 ts(("LO", k * 2048 + d, k * 2048 + nc * 16, 16), ls, float(d + 1), ALU.is_equal)
+            tt(hs, (bank, 0, nt * 24, 3), mk, ALU.mult)
+            for d in range(8):
+                ts(("HI", k * 1024 + d, k * 1024 + nc * 8, 8), hs, float(d + 1), ALU.is_equal)
             mm([(("HP", 0, 64), ("LO", k * 2048 + u * 128, k * 2048 + u * 128 + 128), ("HI", k * 1024 + u * 64, k * 1024 + u * 64 + 64),
                  k == 0 and u == 0, 16 * k + u == tiles - 1) for u in range(nt)])
-        tt(v1, ("HP", 0, 64), DG, ALU.mult)
-        tt(a1, sub(v1, 0, 32), sub(v1, 32, 64), ALU.add)
-        tt(a2, sub(a1, 0, 16), sub(a1, 16, 32), ALU.add)
-        tt(VE, sub(a2, 0, 8), sub(a2, 8, 16), ALU.add)
-        tt(DN, VE, UQ, ALU.is_lt)
-        tt(DNB, VE, UQ, ALU.is_lt)
+        copy(HPS, ("HP", 0, 64))
+        op("dve", lambda: g.vector.tensor_tensor(out=ap(DNB), in0=ind(HPS, DL), in1=ap(UQ), op=ALU.is_lt), [HPS, DL, UQ], [DNB], gat(16))
         aps = ("HP", 0, 8)
-        mm([(aps, N16, SENT, True, False), (aps, P16, DNB, False, True)])
+        mm([(aps, N16, SENT, True, False), (aps, P16, sub(DNB, 0, 8), False, True)])
         red(A16, aps, ALU.add)
-        if not last: ts(V16, VB16, A16, ALU.add)
-        tt(to1, DN, VT, ALU.mult)
-        tt(to2, to1, TRW, ALU.add)
+        if not last:
+            for m in (1, 0): ts(sub(SIN, m * 32, m * 32 + 32), sub(SV0, m * 32, m * 32 + 32), A16, ALU.add)
+            ts(V16, VB16, A16, ALU.add)
+        op("dve", lambda: g.vector.tensor_scalar(out=ap(to1), in0=ind(HPS, DL), scalar1=0.5, scalar2=float(W + 128), op0=ALU.is_ge, op1=ALU.mult),
+           [HPS, DL], [to1], gat(16))
+        tt(to2, sub(to1, 0, 8), mo, ALU.add)
         copy(TOFF[pr], to2)
         if not last: scatter(("X", 0, NM), TOFF[pr], ("ZL", t * 128, t * 128 + 128))
-        mm([(("BD", i, 128, 16), ("EI", i * 128, i * 128 + 128), DNB, True, True) for i in range(16)])
+        mm([(("BD", i, 128, 16), ("EI", i * 128, i * 128 + 128), sub(DNB, 0, 8), True, True) for i in range(16)])
         copy(DNR, ("BD", 0, 128))
         nds = ("NDS", t * 128, t * 128 + 128)
         ts(nds, ("BD", 0, 128), -1.0, ALU.mult, 1.0, ALU.add)
@@ -483,20 +500,25 @@ def rank_program(g, core, T, topo):
         krep = []
         for b in range(t + 1):
             for j in range(b * 4, b * 4 + 4):
-                gather("dve" if j in CFG["hg"][t] else "act", ("HG", j * 256, j * 256 + 256), MAP, sub(OFF, j * 16, j * 16 + 16))
+                gather("dve" if j in CFG["hg"][t] else "act", ("HG", j * 256, j * 256 + 256), MAPW, sub(OFF, j * 16, j * 16 + 16))
             tl = [("HG", b * 1024 + k * 128, b * 1024 + k * 128 + 128) for k in range(8)] + ([ndl] if b == t else [])
             kp, kb = ("BD", b * 64, b * 64 + 64), sub(KB, b * 64, b * 64 + 64)
             mm([(kp, x, RHE, n == 0, n == len(tl) - 1) for n, x in enumerate(tl)])
             ts(kb, kp, 0.5, ALU.is_gt, 8.0, ALU.mult)
             if not last: tt(sub(CLX, b * 64, b * 64 + 64), sub(CLX, b * 64, b * 64 + 64), kb, ALU.max)
-            krep.append((("TPB", b * 128, b * 128 + 128), sub(kb, 0, 8), ID, True, True))
+            krep.append((("D0" if last and b > 1 else "TPB", b * 128, b * 128 + 128), sub(kb, 0, 8), ID, True, True))
         if not last: scatter(MAP, MOFF[pr], ZERO)
         mm(krep, p8=True)
         e = 128 * t + 128
-        op("act", lambda e=e: g.scalar.activation(out=T.PB[0:8, KT[1]:KT[1] + e], in_=T.TPB[0:8, 0:e], func=AF.Copy), [("TPB", 0, e)], [sub(KT, 0, e)], dv(e))
-        op("pe", lambda e=e: g.tensor.matmul(T.TPB[:, 0:e], T.PB[0:8, EXP[1]:EXP[2]], T.PB[0:8, KT[1]:KT[1] + e], True, True),
-           [EXP, sub(KT, 0, e)], [("TPB", 0, e)], e * PEC)
-        act(sub(KRP, 0, e), ("TPB", 0, e), AF.Copy)
+        f = e // 2 if last else e
+        op("act", lambda f=f: g.scalar.activation(out=T.PB[0:8, KT[1]:KT[1] + f], in_=T.TPB[0:8, 0:f], func=AF.Copy), [("TPB", 0, f)], [sub(KT, 0, f)], dv(f))
+        if last:
+            op("dve", lambda f=f, e=e: g.vector.tensor_copy(out=T.PB[0:8, KT[1] + f:KT[1] + e], in_=T.D0[0:8, f:e]), [("D0", f, e)], [sub(KT, f, e)], dv(e - f))
+        for bank, lo, hi in ((("TPB", 0, f), ("D0", f, e)) if last else (("TPB", 0, e),)):
+            op("pe", lambda bank=bank, lo=lo, hi=hi: g.tensor.matmul(T[bank][:, lo:hi], T.PB[0:8, EXP[1]:EXP[2]], T.PB[0:8, KT[1] + lo:KT[1] + hi], True, True),
+               [EXP, sub(KT, lo, hi)], [(bank, lo, hi)], (hi - lo) * PEC)
+        act(sub(KRP, 0, f), ("TPB", 0, f), AF.Copy)
+        if last: copy(sub(KRP, f, e), ("D0", f, e))
         for h in range(2): gather("dve" if CFG["lg"] == h else "act", sub(LG, h * 256, h * 256 + 256), KRP, sub(LRU[pr], h * 16, h * 16 + 16))
         bw = ("BD", 384, 416)
         mm([(bw, sel(i), sub(LG, i, 512, 16), i == 0, i == 15) for i in range(16)])

from concourse.mybir import AluOpType as ALU, AxisListType, ActivationFunctionType as AF

W, L, TS = 8192, 512, 4
KS = (3, 29)
NM = 16384 + 256

SCRATCH = {
    "X": ("sbuf", [128, NM], "bfloat16"), "MAP": ("sbuf", [128, NM], "bfloat16"),
    "SEL": ("sbuf", [128, 2048], "bfloat16"), "EI": ("sbuf", [128, 2048], "bfloat16"),
    "SD": ("sbuf", [128, 512], "bfloat16"), "V0": ("sbuf", [128, 32], "int32"), "THI": ("sbuf", [128, 4], "int32"),
    "KL": ("sbuf", [128, 512], "float32"), "KWS": ("sbuf", [128, 32], "float32"), "KWL": ("sbuf", [128, 32], "float32"),
    "ZS": ("sbuf", [128, 384], "bfloat16"), "ZL": ("sbuf", [128, 384], "bfloat16"),
    "NDS": ("sbuf", [128, 512], "bfloat16"), "NDL": ("sbuf", [128, 512], "bfloat16"),
    "MVS": ("sbuf", [128, 512], "bfloat16"), "MVL": ("sbuf", [128, 512], "bfloat16"),
    "G": ("sbuf", [128, 4096], "bfloat16"), "HG": ("sbuf", [128, 4096], "bfloat16"),
    "LO": ("sbuf", [128, 4096], "bfloat16"), "HI": ("sbuf", [128, 2048], "bfloat16"),
    "KX": ("sbuf", [128, 512], "float32"), "KEYR": ("sbuf", [128, 512], "float32"),
    "YT": ("sbuf", [128, 256], "float32"), "YS": ("sbuf", [128, 64], "float32"),
    "PF": ("sbuf", [128, 6000], "float32"), "PI": ("sbuf", [128, 3000], "int32"),
    "PU": ("sbuf", [128, 1000], "uint16"), "PB": ("sbuf", [128, 12000], "bfloat16"),
}
for _t in range(TS): SCRATCH["KSD%d" % _t] = ("sbuf", [128, 1536], "float32")
PSUM = ("U0", "D0", "D1", "D2", "TPA", "TPB", "HP", "BD")
for _b in PSUM: SCRATCH[_b] = ("psum", [128, 512], "float32")
QUEUES = ("pe", "dve", "act", "gp")
SEMAPHORES = (["c_" + q for q in QUEUES] + ["ld_x", "ld_sd", "ld_v", "ld_th", "st_t", "st_s", "lsem"]
              + ["%s%d" % (k, t) for k in ("rk", "rw", "rm", "rz", "rb") for t in range(TS)])

CYC, PEC, HOP = 0.001, 0.00086, 0.16
ORDER = {}
CFG = {"map": ((1, 2), (1, 2, 4, 6), (2, 4, 5, 6, 8), (3, 5, 6, 7, 11, 13)),
       "hg": ((0, 1, 2, 3), (2, 3, 4, 5), (0, 3, 8, 9, 11), (0, 3, 4, 7, 8, 11, 13, 14)),
       "cut": ((0, 8), (8, 16), (16, 24), (24, 32)), "dcut": ((0, 16), (16, 24), (24, 32)),
       "kw": 3, "kx": 8, "lg": 0, "span": [0.0]}


def dv(n, c=1.0):
    return max(64, n * c) * CYC


def gat(n):
    return 0.066 + 1.56 * n * CYC


def sca(n):
    return 0.06 + 3.8 * n * CYC


def rank_program(g, core, T, topo):
    rank = T.rank_of(core)
    if rank is None:
        return
    ops = []
    acc = {}
    pool = {"PF": [0], "PI": [0], "PU": [0], "PB": [0]}

    def op(eng, fn, reads, writes, dur, event=None, after=(), lat=0.0, early=False):
        n = len(ops)
        deps = {}

        def need(m, wait):
            deps[m] = deps.get(m, False) or wait
        for (b, lo, hi) in reads:
            ex = b in PSUM
            for (l2, h2, m, wr) in acc.get(b, []):
                over = l2 < hi and lo < h2
                if over or ex:
                    same = ops[m]["eng"] == eng
                    if wr: need(m, over if same else True)
                    elif ex: need(m, not same)
        for (b, lo, hi) in writes:
            ex = b in PSUM
            for (l2, h2, m, wr) in acc.get(b, []):
                if l2 < hi and lo < h2 or ex:
                    need(m, ops[m]["eng"] != eng or eng in ("sp", "net") or not (wr or ex))
        for m in after: need(m, False)
        ops.append({"eng": eng, "fn": fn, "deps": deps, "dur": dur, "event": event, "lat": lat, "early": early})
        for (b, lo, hi) in reads:
            acc.setdefault(b, []).append((lo, hi, n, False))
        for (b, lo, hi) in writes:
            if b in PSUM: keep = [a for a in acc.get(b, []) if ops[a[2]]["eng"] == eng and a[3]][-40:]
            else: keep = [a for a in acc.get(b, []) if not (lo <= a[0] and a[1] <= hi)]
            acc[b] = keep + [(lo, hi, n, True)]
        return n

    def al(p, n):
        a = pool[p][0]
        pool[p][0] = a + (n + 15) // 16 * 16
        assert pool[p][0] <= SCRATCH[p][1][1], p
        return (p, a, a + n)

    def two(p, n):
        return (al(p, n), al(p, n))

    def ap(r):
        return T[r[0]][:, r[1]:r[2]] if len(r) == 3 else T[r[0]][:, r[1]:r[2]:r[3]]

    def rg(r):
        return (r[0], r[1], r[2])

    def sub(r, lo, hi, st=None):
        return (r[0], r[1] + lo, r[1] + hi) if st is None else (r[0], r[1] + lo, r[1] + hi, st)

    def wd(r):
        return r[2] - r[1] if len(r) == 3 else (r[2] - r[1] + r[3] - 1) // r[3]

    def fastc(*rs):
        return 0.5 if all(SCRATCH[r[0]][2] in ("bfloat16", "uint16") and r[0] not in PSUM for r in rs) else 1.0

    def copy(o, i):
        op("dve", lambda: g.vector.tensor_copy(out=ap(o), in_=ap(i)), [rg(i)], [rg(o)], dv(wd(o), fastc(o, i)))

    def tt(o, a, b, f):
        c = 1.0 if (a[0] in PSUM or b[0] in PSUM) else 2.0
        op("dve", lambda: g.vector.tensor_tensor(out=ap(o), in0=ap(a), in1=ap(b), op=f), [rg(a), rg(b)], [rg(o)], dv(wd(o), c))

    def ts(o, a, s1, f1, s2=None, f2=None):
        rd = [rg(a)] + [rg(s) for s in (s1, s2) if isinstance(s, tuple)]

        def fn():
            x1 = ap(s1) if isinstance(s1, tuple) else s1
            x2 = ap(s2) if isinstance(s2, tuple) else s2
            if f2 is None:
                return g.vector.tensor_scalar(out=ap(o), in0=ap(a), scalar1=x1, scalar2=None, op0=f1)
            return g.vector.tensor_scalar(out=ap(o), in0=ap(a), scalar1=x1, scalar2=x2, op0=f1, op1=f2)
        op("dve", fn, rd, [rg(o)], dv(wd(o), fastc(o, a)))

    def fill(o, v):
        op("dve", lambda: g.vector.memset(ap(o), v), [], [rg(o)], dv(wd(o), fastc(o)), early=128 < wd(o))

    def red(o, a, f):
        op("dve", lambda: g.vector.tensor_reduce(out=ap(o), in_=ap(a), axis=AxisListType.X, op=f), [rg(a)], [rg(o)], dv(wd(a)))

    def ind(win, off):
        return T[win[0]][:, win[1]:win[2]].indirect(ap(off))

    def scatter(win, off, src):
        op("dve", lambda: g.vector.tensor_copy(out=ind(win, off), in_=ap(src)), [rg(off), rg(src)], [rg(win)], sca(wd(src)))

    def gather(eng, o, win, off):
        if eng == "act": fn = lambda: g.scalar.activation(out=ap(o), in_=ind(win, off), func=AF.Copy)
        else: fn = lambda: g.vector.tensor_copy(out=ap(o), in_=ind(win, off))
        op(eng, fn, [rg(win), rg(off)], [rg(o)], gat(wd(o)))

    def act(o, a, f, bias=None, scale=None, acc_o=None):
        rd = [rg(a)] + [rg(r) for r in (bias, scale) if r is not None]

        def fn():
            kw = {}
            if bias is not None: kw["bias"] = ap(bias)
            if scale is not None: kw["scale"] = ap(scale)
            if acc_o is not None: kw["accum_out"] = ap(acc_o)
            return g.scalar.activation(out=ap(o), in_=ap(a), func=f, **kw)
        op("act", fn, rd, [rg(o)] + ([rg(acc_o)] if acc_o is not None else []), dv(wd(o)) + (0.02 if acc_o is not None else 0.0))

    def mm(lst, f32=False, p8=False):
        rd, wr = [], []
        d = 0.0
        for (o, a, b, s0, s1) in lst:
            for r in (a, b):
                if rg(r) not in rd: rd.append(rg(r))
            if rg(o) not in wr: wr.append(rg(o))
            d += max(min(64, wd(a)), wd(b)) * PEC * (4 if f32 else 1)

        def fn():
            x = None
            for (o, a, b, s0, s1) in lst:
                x = g.tensor.matmul(T[o[0]][0:8, o[1]:o[2]] if p8 else ap(o), ap(a), ap(b), s0, s1)
            return x
        op("pe", fn, rd, wr, d)

    def iota(o, pat, base, cm):
        op("gp", lambda: g.iota(ap(o), pat, base, cm, allow_small_or_imprecise_dtypes=True), [], [rg(o)], 0.15 + 2 * wd(o) * CYC)

    def asel(o, a, pat, cmp, base, cm):
        op("gp", lambda: g.affine_select(ap(o), ap(a), pat, cmp, 0.0, base, cm), [rg(a)], [rg(o)], 0.2 + 2 * wd(o) * CYC)

    used = [0]

    def send(dst, o, i, sem, lat):
        rid, pid, _ = topo.addr(dst)
        en = topo.engines(core, dst)[::2]
        m = sum(1 << e for e in en)
        used[0] += len(en)

        def fn():
            g.remote_dma(ap(o), ap(i), T.sem[sem], T.sem.lsem, pid, rid, m)
        s = op("gp", fn, [rg(i)], [], 0.1)
        op("net", None, [], [rg(o)], 0.0, event=(sem, len(en)), after=(s,), lat=lat)

    def dma(o_ap, i_ap, rd, wr, sem, lat, eng="sp"):
        op(eng, lambda: (g.sync if eng == "sp" else g.scalar).dma_start(o_ap, i_ap).then_inc(T.sem[sem], 16), rd, wr, 0.1, event=(sem, 16), lat=lat)

    V0, THI, SD, XW = ("V0", 0, 32), ("THI", 0, 4), ("SD", 0, 512), ("X", 0, W)
    dma(T.V0[:], T.v0[:], [], [V0], "ld_v", 2.0, "act")
    dma(T.THI[:], T.th[:], [], [THI], "ld_th", 3.0, "act")
    dma(T.SD[:], T.sd[:], [], [SD], "ld_sd", 2.5)
    dma(T.X[:, 0:W], T.x[:], [], [XW], "ld_x", 10.0)

    ONE, BO, t0, ID = al("PB", 128), al("PB", 128), al("PB", 128), al("PB", 128)
    fill(ONE, 1.0)
    asel(t0, ONE, [[-16, 8], [0, 16]], ALU.is_ge, 0, 1)
    asel(BO, t0, [[16, 8], [0, 16]], ALU.is_ge, 15, -1)
    asel(ID, ONE, [[-1, 128]], ALU.is_equal, 0, 1)
    fill(("SEL", 0, 2048), 0.0)
    for i in range(16): copy(("SEL", i * 128 + i, (i + 1) * 128, 16), sub(BO, i, 128, 16))

    def sel(i):
        return ("SEL", i * 128, (i + 1) * 128)
    NID, NID16 = al("PB", 128), al("PB", 128)
    ts(NID, ID, -1.0, ALU.mult)
    ts(NID16, ID, -16.0, ALU.mult)
    BIAS = (al("PF", 1), al("PF", 1))
    for m in range(2): fill(BIAS[m], 8.0 * KS[m])
    h1, h2, M16 = al("PF", 64), al("PF", 32), al("PF", 16)
    tt(h1, sub(ID, 0, 64), sub(ID, 64, 128), ALU.add)
    tt(h2, sub(h1, 0, 32), sub(h1, 32, 64), ALU.add)
    tt(M16, sub(h2, 0, 16), sub(h2, 16, 32), ALU.add)

    def m16(i):
        return sub(M16, i, i + 1)
    i16, x16, IC = al("PF", 16), al("PF", 16), al("PF", 1)
    iota(i16, [[1, 16]], 0, 0)
    tt(x16, M16, i16, ALU.mult)
    red(IC, x16, ALU.add)
    INI, iq, LANE, TL, P16N = al("PF", 1), al("PF", 32), al("PF", 32), al("PF", 32), al("PF", 32)
    ts(INI, IC, 512.0 - 16.0, ALU.add)
    iota(iq, [[16, 32]], 0, 0)
    ts(LANE, iq, IC, ALU.add)
    ts(TL, LANE, 512.0, ALU.add)
    fill(P16N, 16.0)
    V16 = al("PF", 64)

    def v16ops(dst, src):
        for m in range(2): ts(sub(dst, m * 32, m * 32 + 32), src, 16.0, ALU.mult, -64.0 * KS[m] ** 2, ALU.add)
    v16ops(V16, V0)

    def sums(zr, extra=None):
        o = ("U0", 0, 32)
        lst = [(o, NID16, extra, True, False)] if extra is not None else []
        for i in range(16): lst.append((o, sel(i), sub(zr, i, 512, 16), extra is None and i == 0, i == 15))
        mm(lst)
        return o
    SQ0 = al("PF", 64)
    o = sums(SD)
    for m in range(2): act(sub(SQ0, m * 32, m * 32 + 32), o, AF.Square, BIAS[m])

    MAP, MAPW = ("MAP", 0, NM), ("MAP", 0, W)
    fill(MAPW, 0.0)
    TH = al("PF", 4)
    copy(TH, THI)
    NEG = al("PF", 1)
    fill(NEG, -1.0)
    TRI, nbo, BOF = al("PB", 128), al("PB", 128), al("PF", 128)
    ts(nbo, BO, -1.0, ALU.mult)
    asel(TRI, nbo, [[-1, 128]], ALU.is_ge, 0, 1)
    copy(BOF, BO)
    for i in range(16): ts(("EI", i * 128, i * 128 + 128), BO, m16(i), ALU.mult)
    RHE, RK = al("PB", 64), al("PB", 24)
    for k in range(8): ts(sub(RHE, k * 8, k * 8 + 8), sub(BO, 0, 128, 16), m16(0), ALU.mult)
    for k in range(3): ts(sub(RK, k, 24, 3), sub(BO, 0, 128, 16), m16(k), ALU.mult)
    ex0, EXP, KT = al("PB", 128), al("PB", 128), al("PB", 512)
    asel(ex0, ONE, [[1, 128]], ALU.is_ge, 0, -16)
    asel(EXP, ex0, [[-1, 128]], ALU.is_ge, 15, 16)
    DM, dm1, dm2 = al("PF", 128), al("PF", 16), al("PF", 16)
    ts(dm1, M16, 33554432.0, ALU.mult, -17.0, ALU.add)
    ts(sub(dm2, 1, 16), sub(M16, 0, 15), -1.0, ALU.mult)
    ts(sub(dm2, 0, 1), m16(15), -1.0, ALU.mult)
    for k in range(8): tt(sub(DM, k * 16, k * 16 + 16), dm1, dm2, ALU.add)
    pc, c8, c9, g8, g9, dl = (al("PF", 1) for _ in range(6))
    DL = al("PU", 1)
    iota(pc, [[0, 1]], 0, 1)
    tt(g8, pc, IC, ALU.subtract)
    ts(c8, IC, 7.5, ALU.is_ge, -8.0, ALU.mult)
    tt(c9, c8, IC, ALU.add)
    ts(g9, g8, 0.5, ALU.mult)
    tt(dl, g9, c9, ALU.add)
    copy(DL, dl)
    i8, TRW, SROW = al("PF", 8), al("PF", 8), al("PF", 128)
    iota(i8, [[16, 8]], 2 * W + 128, 0)
    ts(TRW, i8, IC, ALU.add)
    iota(SROW, [[1024, 128]], W * 1024 + 896, 0)
    for t in range(TS): copy(("KSD%d" % t, 0, 128), SROW)
    hir, lor, hm2, lm2, SC = al("PF", 128), al("PF", 128), al("PF", 128), al("PF", 128), al("PB", 128)
    iota(hir, [[1, 8], [0, 16]], 1, 0)
    iota(lor, [[0, 8], [1, 16]], 1, 0)
    ts(hm2, hir, m16(0), ALU.mult)
    ts(lm2, lor, m16(1), ALU.mult)
    tt(SC, hm2, lm2, ALU.add)
    KRP, P16, N16, ZERO = al("PB", 512), al("PB", 128), al("PB", 128), al("PB", 128)
    fill(KRP, 0.0)
    fill(P16, 16.0)
    fill(N16, -16.0)
    fill(ZERO, 0.0)

    SQ, SI, C16, Y1, HB = two("PF", 64), two("PI", 64), two("PU", 64), two("PB", 512), two("PB", 512)
    ZH, ZF, GE = al("PB", 1536), al("PB", 512), al("PB", 512)
    CN, TM = two("PI", 256), two("PF", 256)
    tda, tdb = al("PF", 256), al("PF", 256)
    OFF, CLX = al("PU", 256), al("PF", 256)
    ZG, SQS, VSE, SIS, CS, VSW = al("PB", 512), al("PF", 64), al("PF", 64), al("PI", 64), al("PI", 64), al("PI", 8)
    KSI, KSC, CLB, MK = al("PI", 128), al("PI", 128), al("PB", 128), al("PB", 128)
    LRF, lr1, lr2, lr3, LRU = two("PF", 32), al("PF", 32), al("PF", 32), al("PF", 32), two("PU", 32)
    KB, LG, WO = al("PB", 256), al("PB", 512), two("PF", 32)
    HALT, GO, FRA, FR = al("PB", 32), al("PB", 32), al("PB", 32), two("PB", 32)
    scn, HT, wy, SOFF = al("PF", 32), al("PF", 32), al("PF", 32), al("PU", 32)
    vm, vq, vs, v37, vsum, vbp = (al("PI", 32) for _ in range(6))
    SV0, SIN = al("PF", 64), al("PI", 64)
    VB16, VBL, VN, VNs, VC = al("PF", 64), al("PF", 32), two("PI", 32), al("PI", 32), two("PF", 32)
    vd, vd2, KW, kw1 = al("PF", 32), al("PF", 32), al("PF", 32), al("PF", 32)
    KJ, KM, MN, UQ = al("PF", 128), al("PF", 128), al("PF", 8), al("PF", 16)
    fill(UQ, 0.0)
    AB = [al("PF", 16 * q + 16) for q in range(8)]
    KI, VW, VT = al("PI", 8), al("PI", 8), al("PF", 8)
    mt, mo, to1, to2 = al("PF", 8), al("PF", 8), al("PF", 16), al("PF", 8)
    MOFF, TOFF = two("PU", 8), two("PU", 8)
    MG = al("PB", 128)
    ZI, ZJ, ZO, DNR = al("PI", 8), al("PI", 8), al("PU", 8), al("PB", 128)
    HS, LS = two("PB", 128), two("PB", 128)
    HPS, DNB, SENT, A16 = al("PF", 64), al("PB", 16), al("PB", 8), al("PF", 1)

    def vbase(src):
        copy(vs, src)
        ts(vm, vs, 4095, ALU.bitwise_and)
        tt(vq, vm, vm, ALU.mult)
        ts(vsum, vq, 3, ALU.arith_shift_right)
        ts(v37, vs, 37.0, ALU.mult)
        tt(vsum, vsum, v37, ALU.add)
        ts(vbp, vsum, 8191, ALU.bitwise_and)
        ts(VBL, vbp, 16.0, ALU.mult)
        v16ops(VB16, vbp)
        tt(SV0, SQ0, VB16, ALU.add)

    def keys(v):
        ts(kw1, v, 1024.0, ALU.mult)
        tt(KW, kw1, LANE, ALU.add)
        for i in range(16):
            if i < CFG["kx"]: act(("KX", i, 512, 16), KW, AF.Copy, scale=m16(i))
            else: ts(("KX", i, 512, 16), KW, m16(i), ALU.mult)
        for k in range(4): mm([(("TPA", k * 128, k * 128 + 128), BOF, ("KX", k * 128, k * 128 + 128), True, True)], f32=True)
        act(("KEYR", 0, 512), ("TPA", 0, 512), AF.Copy)

    copy(VC[0], V0)
    keys(V0)
    vbase(VC[0])

    for t in range(TS):
        pr, nx, last = t % 2, (t + 1) % 2, t == TS - 1
        partner = T.cores[rank ^ (1 + t % 7)]
        cn, fr, vc = CN[pr], FR[pr], VC[pr]
        zc = SD
        for b in range(4):
            p = b % 2
            if b == 0: sq = SQ0
            else:
                sq = SQ[p]
                o = sums(zc)
                for m in (1, 0): act(sub(sq, m * 32, m * 32 + 32), o, AF.Square, BIAS[m])
            c16 = C16[p]
            for m in (1, 0):
                k0, k1 = m * 32, m * 32 + 32
                if b or not t: tt(sub(SI[p], k0, k1), sub(sq, k0, k1), sub(V16, k0, k1), ALU.add)
                c = sub(cn, b * 64 + k0, b * 64 + k1)
                ts(c, sub(SI[p] if b or not t else SIN, k0, k1), 4, ALU.arith_shift_right, 8191, ALU.bitwise_and)
                copy(sub(c16, k0, k1), c)
            zn = sub(ZH, b * 512, b * 512 + 512) if b < 3 else ZF
            for c0, c1 in CFG["cut"]:
                yy, hu = sub(Y1[p], c0 * 16, c1 * 16), sub(HB[p], c0 * 16, c1 * 16)
                gather("act", yy, XW, sub(c16, 32 + c0, 32 + c1))
                o16 = sub(c16, c0, c1)
                op("dve", lambda o16=o16, yy=yy, hu=hu: g.vector.tensor_tensor(out=ap(hu), in0=ind(XW, o16), in1=ap(yy), op=ALU.max),
                   [XW, o16, yy], [hu], gat(c1 * 16 - c0 * 16))
            for h, (c0, c1) in enumerate(CFG["dcut"]):
                r0, r1 = c0 * 16, c1 * 16
                dps = ("D%d" % h, 0, r1 - r0)
                mm([(dps, NID, sub(zc, r0, r1), True, False)])
                mm([(dps, ID, sub(HB[p], r0, r1), False, True)])
                act(sub(zn, r0, r1), dps, AF.Abs)
            zc = zn
        if t:
            mm([(("TPB", k * 32, k * 32 + 32), ID, fr, True, True) for k in range(8)])
            tt(tda, TM[nx] if t > 1 else CN[0], cn, ALU.subtract)
            tt(tdb, ("TPB", 0, 256), tda, ALU.mult)
            tt(("YT", 0, 256) if last else TM[pr], tdb, cn, ALU.add)
        for c0, c1 in CFG["dcut"]: ts(sub(GE, c0 * 16, c1 * 16), sub(zc, c0 * 16, c1 * 16), sub(TH, t, t + 1), ALU.is_ge)
        o = sums(GE, fr if t else None)
        ts(HALT, o, 8.5, ALU.is_ge)
        p2, p12 = ("HP", 0, 32), ("HP", 32, 64)
        mm([(p2, BO, HALT, True, True), (p12, TRI, HALT, True, True)])
        tt(HT, HALT, TL, ALU.mult)
        op("dve", lambda p2=p2: g.vector.tensor_tensor_scan(out=ap(scn), data0=ap(P16N), data1=ap(p2), initial=ap(INI), op0=ALU.add, op1=ALU.add),
           [P16N, p2, INI], [scn], dv(32))
        tt(wy, p12, HT, ALU.subtract)
        tt(WO[pr], wy, scn, ALU.add)
        copy(SOFF, WO[pr])
        scatter(("KSD%d" % t, 0, 1536), SOFF, ("KEYR", 0, 512))
        ks = ("KSD%d" % t, 0, 128)
        send(partner, ("KL", t * 128, t * 128 + 128), ks, "rk%d" % t, 2.4)
        kws = ("KWS", t * 8, t * 8 + 8)
        tt(KM, ks, DM, ALU.min)
        for q in range(8):
            if q < CFG["kw"]: act(sub(KJ, q * 16, q * 16 + 16), sub(KM, q * 16, q * 16 + 16), AF.Copy, acc_o=sub(kws, q, q + 1))
            else: red(sub(kws, q, q + 1), sub(KM, q * 16, q * 16 + 16), ALU.add)
        send(partner, ("KWL", t * 8, t * 8 + 8), kws, "rw%d" % t, 1.8)
        copy(KSI, ks)
        ts(KSC, KSI, 7, ALU.arith_shift_right, 7, ALU.bitwise_and)
        mvs = ("MVS", t * 128, t * 128 + 128)
        ts(MG, KSC, 1.0, ALU.add, m16(2), ALU.mult)
        tt(mvs, MG, SC, ALU.add)
        send(partner, ("MVL", t * 128, t * 128 + 128), mvs, "rm%d" % t, 2.2)
        ts(GO, WO[pr], 127.5, ALU.is_lt)
        if t:
            tt(FRA, fr, GO, ALU.add)
            tt(lr1, WO[pr], LRF[nx], ALU.subtract)
            ts(lr2, lr1, 128.0 * t, ALU.add)
            tt(lr3, lr2, GO, ALU.mult)
            tt(LRF[pr], LRF[nx], lr3, ALU.add)
        else:
            copy(FRA, GO)
            tt(LRF[pr], WO[pr], GO, ALU.mult)
        copy(LRU[pr], LRF[pr])
        ts(ZI, kws, 256.0, ALU.add)
        ts(ZJ, ZI, 511, ALU.bitwise_and)
        copy(ZO, ZJ)
        for b in range(4):
            gather("act", sub(ZG, b * 128, b * 128 + 128), SD if b == 0 else sub(ZH, b * 512 - 512, b * 512), ZO)
        us = ("BD", 0, 32)
        mm([(us, sel(i), sub(ZG, i, 512, 16), i == 0, i == 15) for i in range(16)])
        for m in range(2): act(sub(SQS, m * 32, m * 32 + 32), us, AF.Square, BIAS[m])
        ts(VSW, ZI, 10, ALU.arith_shift_right, 8191, ALU.bitwise_and)
        ts(sub(VSE, 0, 8), VSW, 16.0, ALU.mult, -64.0 * KS[0] ** 2, ALU.add)
        copy(sub(VSE, 8, 16), sub(VSE, 0, 8))
        copy(sub(VSE, 16, 32), sub(VSE, 0, 16))
        ts(sub(VSE, 32, 64), sub(VSE, 0, 32), 64.0 * (KS[0] ** 2 - KS[1] ** 2), ALU.add)
        tt(SIS, SQS, VSE, ALU.add)
        ts(CS, SIS, 4, ALU.arith_shift_right, 8191, ALU.bitwise_and)
        copy(sub(OFF, t * 64, t * 64 + 64), CS)
        ts(CLB, KSC, 1.0, ALU.add)
        mm([(("BD", 64, 128), CLB, RHE, True, True)])
        copy(sub(CLX, t * 64, t * 64 + 64), ("BD", 64, 128))
        if not last:
            gather("act", ("ZS", t * 128, t * 128 + 128), ZF, ZO)
            send(partner, ("ZL", t * 128, t * 128 + 128), ("ZS", t * 128, t * 128 + 128), "rz%d" % t, 2.2)
        kl, kwl = ("KL", t * 128, t * 128 + 128), ("KWL", t * 8, t * 8 + 8)
        for q in range(8): act(AB[q], sub(kl, 0, 16 * q + 16), AF.Abs, sub(kwl, q, q + 1), NEG)
        ts(KI, kwl, 256.0, ALU.add)
        ts(VW, KI, 10, ALU.arith_shift_right)
        tt(VT, VW, TRW, ALU.subtract)
        ts(SENT, kwl, float(W * 1024), ALU.is_ge)
        for q in range(8): red(sub(MN, q, q + 1), AB[q], ALU.min)
        uq = sub(UQ, 0, 8)
        ts(uq, MN, 255.5, ALU.is_ge)
        tt(mt, uq, VT, ALU.mult)
        tt(mo, mt, TRW, ALU.add)
        copy(MOFF[pr], mo)
        scatter(MAP, MOFF[pr], ("MVL", t * 128, t * 128 + 128))
        tiles = 8 * (t + 1)
        for k in range((t + 2) // 2):
            bank = ("TPA", "TPB")[k]
            nt = min(16, tiles - 16 * k)
            for j in range(nt // 2):
                jj = k * 8 + j
                gather("dve" if jj in CFG["map"][t] else "act", ("G", jj * 256, jj * 256 + 256), MAPW, sub(OFF, jj * 16, jj * 16 + 16))
                mm([((bank, (2 * j + w) * 24, (2 * j + w) * 24 + 24), ("G", jj * 256 + w * 128, jj * 256 + w * 128 + 128), RK, True, True) for w in range(2)])
            nc = nt * 8
            hs, ls, mk = sub(HS[k], 0, nc), sub(LS[k], 0, nc), sub(MK, 0, nc)
            copy(ls, (bank, 1, nt * 24, 3))
            tt(mk, (bank, 2, nt * 24, 3), sub(CLX, k * 128, k * 128 + nc), ALU.is_ge)
            for d in range(16):
                ts(("LO", k * 2048 + d, k * 2048 + nc * 16, 16), ls, float(d + 1), ALU.is_equal)
            tt(hs, (bank, 0, nt * 24, 3), mk, ALU.mult)
            for d in range(8):
                ts(("HI", k * 1024 + d, k * 1024 + nc * 8, 8), hs, float(d + 1), ALU.is_equal)
            mm([(("HP", 0, 64), ("LO", k * 2048 + u * 128, k * 2048 + u * 128 + 128), ("HI", k * 1024 + u * 64, k * 1024 + u * 64 + 64),
                 k == 0 and u == 0, 16 * k + u == tiles - 1) for u in range(nt)])
        copy(HPS, ("HP", 0, 64))
        op("dve", lambda: g.vector.tensor_tensor(out=ap(DNB), in0=ind(HPS, DL), in1=ap(UQ), op=ALU.is_lt), [HPS, DL, UQ], [DNB], gat(16))
        aps = ("HP", 0, 8)
        mm([(aps, N16, SENT, True, False), (aps, P16, sub(DNB, 0, 8), False, True)])
        red(A16, aps, ALU.add)
        if not last:
            for m in (1, 0): ts(sub(SIN, m * 32, m * 32 + 32), sub(SV0, m * 32, m * 32 + 32), A16, ALU.add)
            ts(V16, VB16, A16, ALU.add)
        op("dve", lambda: g.vector.tensor_scalar(out=ap(to1), in0=ind(HPS, DL), scalar1=0.5, scalar2=float(W + 128), op0=ALU.is_ge, op1=ALU.mult),
           [HPS, DL], [to1], gat(16))
        tt(to2, sub(to1, 0, 8), mo, ALU.add)
        copy(TOFF[pr], to2)
        if not last: scatter(("X", 0, NM), TOFF[pr], ("ZL", t * 128, t * 128 + 128))
        mm([(("BD", i, 128, 16), ("EI", i * 128, i * 128 + 128), sub(DNB, 0, 8), True, True) for i in range(16)])
        copy(DNR, ("BD", 0, 128))
        nds = ("NDS", t * 128, t * 128 + 128)
        ts(nds, ("BD", 0, 128), -1.0, ALU.mult, 1.0, ALU.add)
        scatter(MAP, MOFF[pr], DNR)
        ndl = ("NDL", t * 128, t * 128 + 128)
        send(partner, ndl, nds, "rb%d" % t, 2.0)
        vn = VN[pr]
        ts(VNs, VBL, A16, ALU.add)
        ts(vn, VNs, 4, ALU.arith_shift_right, 8191, ALU.bitwise_and)
        if not last: keys(vn)
        krep = []
        for b in range(t + 1):
            for j in range(b * 4, b * 4 + 4):
                gather("dve" if j in CFG["hg"][t] else "act", ("HG", j * 256, j * 256 + 256), MAPW, sub(OFF, j * 16, j * 16 + 16))
            tl = [("HG", b * 1024 + k * 128, b * 1024 + k * 128 + 128) for k in range(8)] + ([ndl] if b == t else [])
            kp, kb = ("BD", b * 64, b * 64 + 64), sub(KB, b * 64, b * 64 + 64)
            mm([(kp, x, RHE, n == 0, n == len(tl) - 1) for n, x in enumerate(tl)])
            ts(kb, kp, 0.5, ALU.is_gt, 8.0, ALU.mult)
            if not last: tt(sub(CLX, b * 64, b * 64 + 64), sub(CLX, b * 64, b * 64 + 64), kb, ALU.max)
            krep.append((("D0" if last and b > 1 else "TPB", b * 128, b * 128 + 128), sub(kb, 0, 8), ID, True, True))
        if not last: scatter(MAP, MOFF[pr], ZERO)
        mm(krep, p8=True)
        e = 128 * t + 128
        f = e // 2 if last else e
        op("act", lambda f=f: g.scalar.activation(out=T.PB[0:8, KT[1]:KT[1] + f], in_=T.TPB[0:8, 0:f], func=AF.Copy), [("TPB", 0, f)], [sub(KT, 0, f)], dv(f))
        if last:
            op("dve", lambda f=f, e=e: g.vector.tensor_copy(out=T.PB[0:8, KT[1] + f:KT[1] + e], in_=T.D0[0:8, f:e]), [("D0", f, e)], [sub(KT, f, e)], dv(e - f))
        for bank, lo, hi in ((("TPB", 0, f), ("D0", f, e)) if last else (("TPB", 0, e),)):
            op("pe", lambda bank=bank, lo=lo, hi=hi: g.tensor.matmul(T[bank][:, lo:hi], T.PB[0:8, EXP[1]:EXP[2]], T.PB[0:8, KT[1] + lo:KT[1] + hi], True, True),
               [EXP, sub(KT, lo, hi)], [(bank, lo, hi)], (hi - lo) * PEC)
        act(sub(KRP, 0, f), ("TPB", 0, f), AF.Copy)
        if last: copy(sub(KRP, f, e), ("D0", f, e))
        for h in range(2): gather("dve" if CFG["lg"] == h else "act", sub(LG, h * 256, h * 256 + 256), KRP, sub(LRU[pr], h * 16, h * 16 + 16))
        bw = ("BD", 384, 416)
        mm([(bw, sel(i), sub(LG, i, 512, 16), i == 0, i == 15) for i in range(16)])
        frn = FR[nx]
        tt(frn, FRA, bw, ALU.is_gt)
        vcn = ("YS", 0, 32) if last else VC[nx]
        tt(vd, vc, vn, ALU.subtract)
        tt(vd2, vd, frn, ALU.mult)
        tt(vcn, vd2, vn, ALU.add)
        if not last: vbase(vcn)

    dma(T.yt[:], T.YT[:], [("YT", 0, 256)], [], "st_t", 2.0)
    copy(("YS", 32, 64), FR[TS % 2])
    dma(T.ys[:], T.YS[:], [("YS", 0, 64)], [], "st_s", 2.0)

    n = len(ops)
    if n not in ORDER:
        users = [[] for _ in range(n)]
        for i, o in enumerate(ops):
            for d in o["deps"]: users[d].append(i)
        pri = [0.0] * n
        for i in range(n - 1, -1, -1):
            best = 0.0
            for u in users[i]: best = max(best, pri[u] + (HOP if ops[u]["deps"][i] else 0.0))
            pri[i] = best + ops[i]["dur"] + ops[i]["lat"]
            if ops[i]["early"]: pri[i] = 400.0 + pri[i] * 0.01
        busy = {}
        start = [0.0] * n
        left = [len(o["deps"]) for o in ops]
        ready = [i for i in range(n) if left[i] == 0]
        while ready:
            i = max(ready, key=lambda j: (pri[j], -j))
            ready.remove(i)
            o = ops[i]
            at = 0.0
            for d, w in o["deps"].items():
                e = start[d] + ops[d]["dur"]
                at = max(at, e + ops[d]["lat"] + HOP if w else e)
            if o["eng"] != "net":
                sl = busy.setdefault(o["eng"], [])
                k = len(sl)
                while k > 0 and sl[k - 1][1] > at: k -= 1
                while k < len(sl) and sl[k][0] < at + o["dur"] - 1e-9:
                    at = max(at, sl[k][1])
                    k += 1
                sl.insert(k, (at, at + o["dur"]))
            start[i] = at
            CFG["span"][0] = max(CFG["span"][0], at + o["dur"] + o["lat"])
            for u in users[i]:
                left[u] -= 1
                if left[u] == 0: ready.append(u)
        ORDER[n] = sorted(range(n), key=lambda i: (start[i], i))
    order = ORDER[n]

    pos, cnt = {}, {}
    for i in order:
        q = ops[i]["eng"]
        cnt[q] = cnt.get(q, 0) + 1
        pos[i] = cnt[q]
    known, vcs, waits, needed, final = {}, {}, {}, set(), {}
    for i in order:
        o = ops[i]
        q = o["eng"]
        final[q] = i
        if q == "net":
            vcs[i] = {("ev", i): 1}
            continue
        kn = known.setdefault(q, {})
        mine = []
        for d in sorted((d for d, w in o["deps"].items() if w), key=lambda d: -pos[d]):
            key, val = (("ev", d), 1) if ops[d]["event"] else (ops[d]["eng"], pos[d])
            if kn.get(key, 0) >= val: continue
            mine.append(d)
            needed.add(d)
            for k2, x2 in vcs[d].items():
                if kn.get(k2, 0) < x2: kn[k2] = x2
        waits[i] = mine
        v = dict(kn)
        v[("ev", i) if o["event"] else q] = 1 if o["event"] else pos[i]
        vcs[i] = v
    for q in ("pe", "dve", "act"): needed.add(final[q])

    eng = {"pe": g.tensor, "dve": g.vector, "act": g.scalar, "gp": g, "sp": g.sync}
    num, tot = {}, {}
    for i in order:
        q = ops[i]["eng"]
        if i in needed and not ops[i]["event"]:
            tot[q] = tot.get(q, 0) + 1
            num[i] = tot[q]
    for i in order:
        o = ops[i]
        q = o["eng"]
        if q == "net": continue
        best = {}
        for d in waits[i]:
            s, v = ops[d]["event"] if ops[d]["event"] else ("c_" + ops[d]["eng"], num[d])
            best[s] = max(best.get(s, 0), v)
        for s in best: eng[q].wait_ge(T.sem[s], best[s])
        x = o["fn"]()
        if i in num: x.then_inc(T.sem["c_" + q], 1)
    for q in tot: g.sync.wait_ge(T.sem["c_" + q], tot[q])
    g.sync.wait_ge(T.sem.lsem, used[0])
    for s in ("st_t", "st_s"): g.sync.wait_ge(T.sem[s], 16)
